import numpy as np
import ml_dtypes


def mxq(x, axis, fmt="e4m3"):
    dtype, down = {"e4m3": (ml_dtypes.float8_e4m3fn, 7), "e5m2": (ml_dtypes.float8_e5m2, 14)}[fmt]
    v = np.moveaxis(np.asarray(x, np.float32).astype(ml_dtypes.bfloat16).astype(np.float64), axis, -1)
    blocks = v.reshape(v.shape[:-1] + (-1, 32))
    amax = np.abs(blocks).max(-1, keepdims=True)
    byte = np.maximum(np.where(amax > 0, np.frexp(amax)[1] - 1 + 127, 0) - down, 1)
    scale = np.exp2(byte - 127.0)
    codes = (blocks / scale).astype(np.float32).astype(dtype).astype(np.float64)
    return np.moveaxis((codes * scale).reshape(v.shape), -1, axis)


WIDE = False


def mx_kscale(k):
    if not WIDE:
        return np.ones(k)
    levels = np.array([10, -10, 5, -5, 0])
    if k % 512:
        return np.exp2(np.random.permutation(np.resize(levels, k // 32))).repeat(32)
    a = np.empty((k // 512, 16))
    for p in range(k // 512):
        a[p, :8] = np.random.permutation(np.resize(levels, 8))
        for g in range(8):
            far = levels[np.abs(levels - a[p, g]) >= 10]
            a[p, g + 8] = far[np.random.randint(len(far))]
    return np.exp2(a.ravel()).repeat(32)


BF16 = ml_dtypes.bfloat16


def bf(x):
    return np.asarray(x, np.float32).astype(BF16)


def f64(x):
    return np.asarray(x).astype(np.float64)


E2M1 = np.array([0.0, 0.5, 1.0, 1.5, 2.0, 3.0, 4.0, 6.0, -0.0, -0.5, -1.0, -1.5, -2.0, -3.0, -4.0, -6.0])


def pack_weight(w, fmt):
    k, n = w.shape
    w = f64(bf(w)).reshape(k // 32, 32, n)
    amax = np.abs(w).max(1)
    if fmt == "e4m3":
        byte = np.frexp(amax)[1] - 1 + 127 - 7
    else:
        mant, ex = np.frexp(amax / 6.0)
        byte = np.where(mant > 0.5, ex, ex - 1) + 127
    byte = np.clip(np.where(amax > 0, byte, 1), 1, 254)
    scaled = (w * np.exp2(127.0 - byte)[:, None, :]).reshape(k, n).astype(np.float32)
    by_word = np.ascontiguousarray(scaled.reshape(k // 512, 128, 4, n).transpose(0, 1, 3, 2))
    if fmt == "e4m3":
        words = by_word.astype(ml_dtypes.float8_e4m3fn).view(np.uint8)
    else:
        c = by_word.astype(ml_dtypes.float4_e2m1fn).view(np.uint8) & 0xF
        words = c[..., 0::2] | (c[..., 1::2] << 4)
    return np.ascontiguousarray(words), np.ascontiguousarray(byte.astype(np.uint8).reshape(k // 512, 16, n))


def unpack_weight(words, scales, fmt):
    g, p, n, _ = words.shape
    if fmt == "e4m3":
        vals = np.ascontiguousarray(words).view(ml_dtypes.float8_e4m3fn).astype(np.float64)
    else:
        nib = np.empty((g, p, n, 4), np.uint8)
        nib[..., 0::2] = words & 0xF
        nib[..., 1::2] = words >> 4
        vals = E2M1[nib]
    vals = vals * np.repeat(np.exp2(scales.astype(np.float64) - 127.0), 8, axis=1)[..., None]
    return vals.transpose(0, 1, 3, 2).reshape(g * 512, n)
def pack4(w):
    words, scales = pack_weight(w, "e2m1")
    return words.reshape(words.shape[0], 128, -1), scales


def unpack4(words, scales):
    return unpack_weight(words.reshape(words.shape[0], 128, -1, 2), scales, "e2m1")


B, D, H, V = 512, 512, 1024, 2048


def sigmoid(v):
    return 1.0 / (1.0 + np.exp(-v))


def draw0():
    s, v, t = mx_kscale(D), mx_kscale(H), mx_kscale(H)
    w_words, w_scales = pack4(np.random.standard_normal((D, 3 * H)) / np.sqrt(D) / s[:, None])
    u_words, u_scales = pack4(np.random.standard_normal((H, 3 * H)) / np.sqrt(H) / v[:, None])
    o_words, o_scales = pack_weight(np.random.standard_normal((H, V)) / np.sqrt(H) / t[:, None], "e4m3")
    return {"x": bf(np.random.standard_normal((B, D)) * s),
            "h": bf(np.tanh(np.random.standard_normal((B, H))) * v),
            "w_words": w_words, "w_scales": w_scales,
            "u_words": u_words, "u_scales": u_scales,
            "bias": bf(0.5 * np.random.standard_normal(3 * H)),
            "bias_c": bf(0.5 * np.random.standard_normal(H)),
            "carry": bf((1.0 + 0.1 * np.random.standard_normal(H)) / v),
            "gain": bf((1.0 + 0.1 * np.random.standard_normal(H)) * t),
            "o_words": o_words, "o_scales": o_scales,
            "bias_o": bf(0.3 * np.random.standard_normal(V))}


def core(x, h, w_words, w_scales, u_words, u_scales, bias, bias_c, carry, gain, o_words, o_scales, bias_o):
    xa = mxq(f64(x), 1, "e4m3") @ unpack4(w_words, w_scales)
    ha = mxq(f64(h), 1, "e4m3") @ unpack4(u_words, u_scales)
    b = f64(bias)
    reset = sigmoid(xa[:, :H] + ha[:, :H] + b[:H])
    update = sigmoid(xa[:, H:2 * H] + ha[:, H:2 * H] + b[H:2 * H])
    cand = np.tanh(xa[:, 2 * H:] + b[2 * H:] + reset * (ha[:, 2 * H:] + f64(bias_c)))
    new = (1.0 - update) * cand + update * (f64(h) * f64(carry))
    y = (mxq(new * f64(gain), 1, "e4m3") @ unpack_weight(o_words, o_scales, "e4m3")) + f64(bias_o)
    return y, new


def e4m3fn_bytes(y):
    return np.clip(np.asarray(y, np.float64), -448.0, 448.0).astype(np.float32).astype(ml_dtypes.float8_e4m3fn).view(np.uint8)


def e4m3fn_values(b):
    return np.asarray(b, np.uint8).view(ml_dtypes.float8_e4m3fn).astype(np.float64)


def setup_inputs():
    d = draw0()
    x0 = np.asarray(d['x']).astype(np.float64)
    s = (np.max(np.abs(x0), axis=(0,), keepdims=True) / 448.0).astype(np.float32)
    out = {}
    for k, v in d.items():
        if k == 'x':
            out['x_bytes'] = e4m3fn_bytes(x0 / s.astype(np.float64))
            out['x_scale'] = s
        else:
            out[k] = v
    return out


def reference(x_bytes, x_scale, h, w_words, w_scales, u_words, u_scales, bias, bias_c, carry, gain, o_words, o_scales, bias_o):
    return core(e4m3fn_values(x_bytes) * x_scale.astype(np.float64), h, w_words, w_scales, u_words, u_scales, bias, bias_c, carry, gain, o_words, o_scales, bias_o)

@@ -1,0 +1,503 @@
+from contextlib import ExitStack
+
+import concourse.mybir as mybir
+from concourse.masks import make_identity
+
+F32 = mybir.dt.float32
+BF16 = mybir.dt.bfloat16
+I32 = mybir.dt.int32
+U32 = mybir.dt.uint32
+U8 = mybir.dt.uint8
+FP8 = mybir.dt.float8_e4m3fn
+E4M3X4 = mybir.dt.float8_e4m3fn_x4
+E2M1X4 = mybir.dt.float4_e2m1fn_x4
+ACT = mybir.ActivationFunctionType
+ALU = mybir.AluOpType
+
+B, D, H, V = 512, 512, 1024, 2048
+P = 128
+MT = B // P
+JT = H // P
+G_OF_H = H // 512
+FLOPS = 2 * B * (D * 3 * H + H * 3 * H + H * V)
+
+
+def tile_gru_candidate_projection_f7_kernel(
+    tc, x_bytes, x_scale, h, w_words, w_scales, u_words, u_scales, bias, bias_c, carry, gain, o_words, o_scales, bias_o, out_0, out_1
+):
+    nc = tc.nc
+    with ExitStack() as ctx:
+        keep = ctx.enter_context(tc.tile_pool(name="keep", bufs=1))
+        work = ctx.enter_context(tc.tile_pool(name="work", bufs=3))
+        ypool = ctx.enter_context(tc.tile_pool(name="ypool", bufs=3))
+        psum = ctx.enter_context(tc.psum_pool(name="psum", bufs=8))
+        ctx.enter_context(tc.manual_schedule())
+
+        def bank(dtype=F32):
+            cols = 512 if dtype == F32 else 1024
+            bank_tile = psum.tile([P, cols], dtype, name="bank", tag="bank")
+            return bank_tile
+
+        ident = keep.tile([P, P], F32, name="ident")
+        ident_bf = keep.tile([P, P], BF16, name="ident_bf")
+        rows = keep.tile([P, P], BF16, name="rows")
+        cols = keep.tile([P, P], F32, name="cols")
+        xs = keep.tile([P, D], F32, name="xs")
+        xb = keep.tile([P, MT, D], U8, name="xb", align_bytes=64)
+        xf = keep.tile([P, MT, D], BF16, name="xf", align_bytes=64)
+        hsb = keep.tile([P, MT, H], BF16, name="hsb", align_bytes=64)
+        wuA = keep.tile([P, 3, 3, 512], U8, name="wuA", align_bytes=256)
+        wuB = keep.tile([P, 3, 3, 1536], U8, name="wuB", align_bytes=256)
+        us = keep.tile([P, 2, 3 * H], U8, name="us", align_bytes=256)
+        ws = keep.tile([P, 3 * H], U8, name="ws", align_bytes=256)
+        ow = keep.tile([P, 2, V * 4], U8, name="ow", align_bytes=256)
+        osc = keep.tile([P, 2, V], U8, name="osc", align_bytes=256)
+        gain_b = keep.tile([P, H], BF16, name="gain_b")
+        bo_b = keep.tile([P, V], BF16, name="bo_b")
+        junk = keep.tile([P, 1], F32, name="junk")
+
+        nc.vector.memset(us[:].rearrange("p g n -> p (g n)").bitcast(I32), 0)
+        nc.vector.memset(ws[:].bitcast(I32), 0)
+        nc.vector.memset(rows[:], 0.0)
+        nc.vector.memset(junk[:], 0.0)
+        nc.vector.memset(osc[:].rearrange("p g n -> p (g n)").bitcast(I32), 0)
+        make_identity(nc, ident[:])
+        nc.gpsimd.tensor_copy(out=ident_bf[:], in_=ident[:])
+        nc.gpsimd.dma_start(out=rows[0:24, :], in_=bias.rearrange("(r c) -> r c", c=P))
+        nc.gpsimd.dma_start(out=rows[24:32, :], in_=bias_c.rearrange("(r c) -> r c", c=P))
+        nc.gpsimd.dma_start(out=rows[32:40, :], in_=carry.rearrange("(r c) -> r c", c=P))
+
+        nc.scalar.dma_start(out=xs[:], in_=x_scale.rearrange("o k -> (o k)").partition_broadcast(P))
+        nc.scalar.activation(out=junk[:], in_=junk[:], func=ACT.Sigmoid)
+
+        def load_wu(dst, lo, hi):
+            for g in range(3):
+                src = u_words[g] if g < 2 else w_words[0]
+                nc.sync.dma_start(out=dst[:, g, :, :], in_=src.rearrange("p (s n) -> p s n", s=3)[:, :, lo:hi])
+
+        h_view = h.rearrange("(m p) d -> p m d", p=P)
+        nc.sync.dma_start(out=hsb[:, 0, :], in_=h_view[:, 0, :])
+        nc.sync.dma_start(out=xb[:], in_=x_bytes.rearrange("(m p) d -> p m d", p=P))
+        nc.sync.dma_start(out=hsb[:, 1, :], in_=h_view[:, 1, :])
+        load_wu(wuA, 0, 512)
+        for q in range(4):
+            nc.sync.dma_start(
+                out=us[32 * q : 32 * q + 4, :, :].bitcast(I32),
+                in_=u_scales[:, 4 * q : 4 * q + 4, :].rearrange("g q n -> q g n").bitcast(I32),
+            )
+        for q in range(4):
+            nc.sync.dma_start(out=ws[32 * q : 32 * q + 4, :].bitcast(I32), in_=w_scales[0, 4 * q : 4 * q + 4, :].bitcast(I32))
+        nc.sync.dma_start(out=hsb[:, 2:4, :], in_=h_view[:, 2:4, :])
+        load_wu(wuB, 512, 2048)
+        nc.sync.dma_start(out=gain_b[:], in_=gain.partition_broadcast(P))
+        nc.sync.dma_start(out=bo_b[:], in_=bias_o.partition_broadcast(P))
+        for q in range(4):
+            nc.sync.dma_start(
+                out=osc[32 * q : 32 * q + 4, :, :].bitcast(I32),
+                in_=o_scales[:, 4 * q : 4 * q + 4, :].rearrange("g q n -> q g n").bitcast(I32),
+            )
+        for g in range(2):
+            for half in range(2):
+                ps = slice(4096 * half, 4096 * half + 4096)
+                nc.sync.dma_start(out=ow[:, g, ps].bitcast(I32), in_=o_words[g].rearrange("p n t -> p (n t)")[:, ps].bitcast(I32))
+
+        hin = keep.tile([P, 2, B, 4], BF16, name="hin", align_bytes=64)
+        xin = keep.tile([P, B, 4], BF16, name="xin", align_bytes=64)
+        hxc = keep.tile([P, 3, B], U32, name="hxc", align_bytes=256)
+        hxs = keep.tile([P, 3, B], U8, name="hxs", align_bytes=256)
+        hin_words = hin[:].rearrange("p g r t -> p g (r t)").bitcast(F32)
+        xin_words = xin[:].rearrange("p r t -> p (r t)").bitcast(F32)
+
+        def scale_x(m):
+            nc.vector.tensor_tensor(out=xf[:, m, :], in0=xb[:, m, :].bitcast(FP8), in1=xs[:], op=ALU.mult)
+
+        def turn_h(m):
+            words = hsb[:, m, :].bitcast(F32)
+            t = bank()
+            for g in range(2):
+                for u in range(2):
+                    i = 2 * g + u
+                    nc.tensor.transpose(t[:, i * P : (i + 1) * P], words[:, 256 * g + u : 256 * (g + 1) : 2], ident[:])
+            return t
+
+        def turn_x(mp):
+            t = bank()
+            for mm in range(2):
+                words = xf[:, 2 * mp + mm, :].bitcast(F32)
+                for u in range(2):
+                    i = 2 * mm + u
+                    nc.tensor.transpose(t[:, i * P : (i + 1) * P], words[:, u:256:2], ident[:])
+            return t
+
+        def lay_h(m, t, copy):
+            dst = hin_words[:, :, m * 256 : (m + 1) * 256].rearrange("p g (r u) -> p g r u", u=2)
+            copy(out=dst, in_=t[:].rearrange("p (g u r) -> p g r u", g=2, u=2))
+
+        def lay_x(mp, t, copy):
+            dst = xin_words[:, mp * 512 : (mp + 1) * 512].rearrange("p (m r u) -> p m r u", m=2, u=2)
+            copy(out=dst, in_=t[:].rearrange("p (m u r) -> p m r u", m=2, u=2))
+
+        def quant_h(m):
+            rs = slice(m * P, (m + 1) * P)
+            for g in range(2):
+                nc.vector.quantize_mx(
+                    out=hxc[:, g, rs].bitcast(E4M3X4), scales=hxs[:, g, rs], in_=hin[:, g, rs, :].rearrange("p r t -> p (r t)")
+                )
+
+        def quant_x(mp):
+            rs = slice(mp * 256, (mp + 1) * 256)
+            nc.vector.quantize_mx(out=hxc[:, 2, rs].bitcast(E4M3X4), scales=hxs[:, 2, rs], in_=xin[:, rs, :].rearrange("p r t -> p (r t)"))
+
+        bias_col = lambda part, j: cols[:, part * JT + j : part * JT + j + 1]
+        PART_BC, PART_CARRY = 3, 4
+
+        def wu_slice(g, s, j):
+            c = j * 256
+            src = wuA[:, g, s, c : c + 256] if j < 2 else wuB[:, g, s, c - 512 : c - 256]
+            return src.bitcast(E2M1X4)
+
+        def gate_mm(out, s, j, groups, rs):
+            c = s * H + j * P
+            for i, g in enumerate(groups):
+                nc.tensor.matmul_mx(
+                    out=out,
+                    lhsT=wu_slice(g, s, j),
+                    lhsT_scale=us[:, g, c : c + P] if g < 2 else ws[:, c : c + P],
+                    rhs=hxc[:, g, rs].bitcast(E4M3X4),
+                    rhs_scale=hxs[:, g, rs],
+                    start=(i == 0),
+                    stop=(i == len(groups) - 1),
+                )
+
+        newo = keep.tile([P, MT, H], F32, name="newo")
+        qb = keep.tile([P, MT, H], BF16, name="qb", align_bytes=64)
+        qin = keep.tile([P, 2, B, 4], BF16, name="qin", align_bytes=64)
+        qc = keep.tile([P, 2, B], U32, name="qc", align_bytes=256)
+        qs = keep.tile([P, 2, B], U8, name="qs", align_bytes=256)
+        qin_words = qin[:].rearrange("p g r t -> p g (r t)").bitcast(F32)
+        new_out = out_1.rearrange("(m p) c -> p m c", p=P)
+        y_out = out_0.rearrange("(m p) v -> p m v", p=P)
+
+        GATES = {"r": (0, (0, 1, 2)), "ch": (2, (0, 1)), "cx": (2, (2,)), "z": (1, (0, 1, 2))}
+
+        class_free = None
+
+        def start_unit(j, m0, nm):
+            u = {"j": j, "m0": m0, "nm": nm, "n": nm * P, "cs": slice(m0 * P, (m0 + nm) * P)}
+            for name in ("r", "z", "t1", "t2", "cand", "d", "e", "new"):
+                made = work.tile([P, B], F32, name=name, tag=name)
+                u[name] = made[:, 0 : u["n"]]
+            return u
+
+        def mm_full(u, names):
+            for name in names:
+                s, groups = GATES[name]
+                t = bank()
+                gate_mm(t[:], s, u["j"], groups, slice(0, B))
+                u["p_" + name] = t[:]
+
+        def mm_tiles(u, names_of_bank, ms):
+            n = u["n"]
+            for names in names_of_bank:
+                if "p_" + names[0] not in u:
+                    t = bank()
+                    for i, name in enumerate(names):
+                        u["p_" + name] = t[:, i * n : (i + 1) * n]
+            for m in ms:
+                k = m - u["m0"]
+                for names in names_of_bank:
+                    for name in names:
+                        s, groups = GATES[name]
+                        gate_mm(u["p_" + name][:, k * P : (k + 1) * P], s, u["j"], groups, slice(m * P, (m + 1) * P))
+
+        def sig(u, name, s):
+            nc.scalar.activation(out=u[name], in_=u["p_" + name], func=ACT.Sigmoid, bias=bias_col(s, u["j"]))
+
+        def cand_in(u):
+            nc.vector.scalar_tensor_tensor(
+                out=u["t1"], in0=u["p_ch"], scalar=bias_col(PART_BC, u["j"]), in1=u["r"], op0=ALU.add, op1=ALU.mult
+            )
+
+        def cand_sum(u):
+            nc.vector.tensor_tensor(out=u["t2"], in0=u["p_cx"], in1=u["t1"], op=ALU.add)
+
+        def cand_tanh(u):
+            nc.scalar.activation(out=u["cand"], in_=u["t2"], func=ACT.Tanh, bias=bias_col(2, u["j"]))
+
+        def turn_state(u):
+            t = bank(BF16)
+            j = u["j"]
+            for k in range(u["nm"]):
+                nc.tensor.transpose(t[:, k * P : (k + 1) * P], hsb[:, u["m0"] + k, j * P : (j + 1) * P], ident_bf[:])
+            u["hT"] = t[:, 0 : u["n"]]
+
+        def state_diff(u):
+            nc.vector.scalar_tensor_tensor(
+                out=u["d"], in0=u["hT"], scalar=bias_col(PART_CARRY, u["j"]), in1=u["cand"], op0=ALU.mult, op1=ALU.subtract
+            )
+
+        def state_gate(u, eng):
+            eng.tensor_tensor(out=u["e"], in0=u["z"], in1=u["d"], op=ALU.mult)
+
+        def state_new(u, eng):
+            eng.tensor_tensor(out=u["new"], in0=u["cand"], in1=u["e"], op=ALU.add)
+
+        def turn_new(u):
+            t = bank()
+            for k in range(u["nm"]):
+                nc.tensor.transpose(t[:, k * P : (k + 1) * P], u["new"][:, k * P : (k + 1) * P], ident[:])
+            u["newT"] = t[:, 0 : u["n"]].rearrange("p (m c) -> p m c", c=P)
+
+        def scale_new(u):
+            cs = slice(u["j"] * P, (u["j"] + 1) * P)
+            nc.vector.tensor_tensor(
+                out=qb[:, u["m0"] : u["m0"] + u["nm"], cs],
+                in0=u["newT"],
+                in1=gain_b[:, cs].unsqueeze(1).to_broadcast([P, u["nm"], P]),
+                op=ALU.mult,
+            )
+
+        def save_new(u, copy):
+            cs = slice(u["j"] * P, (u["j"] + 1) * P)
+            copy(out=newo[:, u["m0"] : u["m0"] + u["nm"], cs], in_=u["newT"])
+
+        def turn_q(g, mp):
+            t = bank()
+            for mm in range(2):
+                words = qb[:, 2 * mp + mm, :].bitcast(F32)
+                for u in range(2):
+                    i = 2 * mm + u
+                    nc.tensor.transpose(t[:, i * P : (i + 1) * P], words[:, 256 * g + u : 256 * (g + 1) : 2], ident[:])
+            return t
+
+        def lay_q(g, mp, t, copy):
+            dst = qin_words[:, g, mp * 512 : (mp + 1) * 512].rearrange("p (m r u) -> p m r u", m=2, u=2)
+            copy(out=dst, in_=t[:].rearrange("p (m u r) -> p m r u", m=2, u=2))
+
+        def quant_q(g, mp):
+            rs = slice(mp * 256, (mp + 1) * 256)
+            nc.vector.quantize_mx(out=qc[:, g, rs].bitcast(E4M3X4), scales=qs[:, g, rs], in_=qin[:, g, rs, :].rearrange("p r t -> p (r t)"))
+
+        def store_new(c0, m0, nm):
+            nc.sync.dma_start(out=new_out[:, m0 : m0 + nm, c0 : c0 + 256], in_=newo[:, m0 : m0 + nm, c0 : c0 + 256])
+
+        def y_mm(m, v, groups, t):
+            for g in groups:
+                nc.tensor.matmul_mx(
+                    out=t[:],
+                    lhsT=qc[:, g, m * P : (m + 1) * P].bitcast(E4M3X4),
+                    lhsT_scale=qs[:, g, m * P : (m + 1) * P],
+                    rhs=ow[:, g, v * 2048 : (v + 1) * 2048].bitcast(E4M3X4),
+                    rhs_scale=osc[:, g, v * 512 : (v + 1) * 512],
+                    start=(g == 0),
+                    stop=(g == 1),
+                )
+
+        def y_add(m, v, t, ys):
+            vs = slice(v * 512, (v + 1) * 512)
+            nc.vector.tensor_tensor(out=ys[:, vs], in0=t[:], in1=bo_b[:, vs], op=ALU.add)
+
+        def y_store(m, v, n, ys):
+            ps = slice(v * 512, (v + n) * 512)
+            nc.sync.dma_start(out=y_out[:, m, ps], in_=ys[:, ps])
+
+        G, VE, SC, VC = nc.gpsimd, nc.vector, nc.scalar.copy, nc.vector.tensor_copy
+        scale_x(0)
+        scale_x(1)
+        t_h0 = turn_h(0)
+        t_x0 = turn_x(0)
+        t_h1 = turn_h(1)
+        lay_h(0, t_h0, SC)
+        lay_x(0, t_x0, VC)
+        lay_h(1, t_h1, SC)
+        quant_h(0)
+        quant_x(0)
+        scale_x(2)
+        quant_h(1)
+        scale_x(3)
+        t_h2 = turn_h(2)
+        t_h3 = turn_h(3)
+        lay_h(2, t_h2, SC)
+        lay_h(3, t_h3, VC)
+        t_x1 = turn_x(1)
+        rows_t = bank(BF16)
+        nc.tensor.transpose(rows_t[:, 0:P], rows[:], ident_bf[:])
+        lay_x(1, t_x1, SC)
+        quant_h(2)
+        quant_h(3)
+        nc.scalar.copy(out=cols[:], in_=rows_t[:, 0:P])
+        quant_x(1)
+        u0 = start_unit(0, 0, 4)
+        FIRST = [("r",), ("ch",), ("cx",), ("z",)]
+        mm_tiles(u0, FIRST, (0, 1))
+        turn_state(u0)
+        mm_tiles(u0, FIRST, (2, 3))
+        sig(u0, "r", 0)
+        cand_in(u0)
+        cand_sum(u0)
+        sig(u0, "z", 1)
+
+        U = {0: u0}
+        for j in range(1, 6):
+            u = start_unit(j, 0, 4)
+            p = U[j - 1]
+            U[j] = u
+            mm_full(u, ("r", "ch", "cx"))
+            cand_tanh(p)
+            state_diff(p)
+            state_gate(p, G)
+            state_new(p, G)
+            sig(u, "r", 0)
+            cand_in(u)
+            cand_sum(u)
+            if j >= 3:
+                turn_new(U[j - 3])
+            turn_state(u)
+            mm_full(u, ("z",))
+            if j >= 3:
+                save_new(U[j - 3], SC)
+                scale_new(U[j - 3])
+            sig(u, "z", 1)
+            if j == 5:
+                store_new(0, 0, 4)
+
+        PAIR = [("r", "ch"), ("cx", "z")]
+        def mm1(u):
+            mm_tiles(u, PAIR[:1], (u["m0"], u["m0"] + 1))
+        def mm2(u):
+            mm_tiles(u, PAIR[1:], (u["m0"], u["m0"] + 1))
+        a6, a7, b6, b7 = start_unit(6, 0, 2), start_unit(7, 0, 2), start_unit(6, 2, 2), start_unit(7, 2, 2)
+        p5 = U[5]
+        mm1(a6)
+        cand_tanh(p5)
+        state_diff(p5)
+        state_gate(p5, G)
+        state_new(p5, G)
+        turn_new(U[3])
+        turn_state(a6)
+        mm2(a6)
+        save_new(U[3], SC)
+        scale_new(U[3])
+        sig(a6, "r", 0)
+        mm1(a7)
+        sig(a6, "z", 1)
+        cand_in(a6)
+        turn_new(U[4])
+        turn_state(a7)
+        mm2(a7)
+        save_new(U[4], SC)
+        cand_sum(a6)
+        sig(a7, "r", 0)
+        scale_new(U[4])
+        store_new(256, 0, 4)
+        mm1(b6)
+        cand_tanh(a6)
+        cand_in(a7)
+        sig(a7, "z", 1)
+        q0a = turn_q(0, 0)
+        q0b = turn_q(0, 1)
+        turn_state(b6)
+        mm2(b6)
+        state_diff(a6)
+        cand_sum(a7)
+        lay_q(0, 0, q0a, SC)
+        state_gate(a6, VE)
+        sig(b6, "r", 0)
+        lay_q(0, 1, q0b, VC)
+        state_new(a6, G)
+        mm1(b7)
+        cand_tanh(a7)
+        cand_in(b6)
+        sig(b6, "z", 1)
+        turn_new(p5)
+        turn_state(b7)
+        mm2(b7)
+        state_diff(a7)
+        cand_sum(b6)
+        save_new(p5, SC)
+        state_gate(a7, VE)
+        sig(b7, "r", 0)
+        quant_q(0, 0)
+        scale_new(p5)
+        state_new(a7, G)
+        quant_q(0, 1)
+        cand_tanh(b6)
+        turn_new(a6)
+        cand_in(b7)
+        sig(b7, "z", 1)
+        state_diff(b6)
+        cand_sum(b7)
+        scale_new(a6)
+        state_gate(b6, VE)
+        ys = {}
+        BY_SCALAR = ((0, 2), (1, 0), (1, 2), (2, 0), (2, 2), (3, 0))
+        banks = {}
+        def y_begin(m, v):
+            t = bank()
+            banks[m, v] = t
+            y_mm(m, v, (0,), t)
+        def y_end(m, v):
+            if (m, v) not in banks:
+                y_begin(m, v)
+            y_mm(m, v, (1,), banks[m, v])
+        def y_evac(m, v):
+            if v == 0:
+                yt = ypool.tile([P, V], F32, name="ys")
+                ys[m] = yt
+            if (m, v) in BY_SCALAR:
+                vs = slice(v * 512, (v + 1) * 512)
+                nc.scalar.copy(out=ys[m][:, vs], in_=banks[m, v][:])
+                nc.gpsimd.tensor_tensor(out=ys[m][:, vs], in0=ys[m][:, vs], in1=bo_b[:, vs], op=ALU.add)
+            else:
+                y_add(m, v, banks[m, v], ys[m])
+            if m == 3 and v >= 2:
+                y_store(m, v, 1, ys[m])
+            elif v % 2 == 1:
+                y_store(m, v - 1, 2, ys[m])
+        y_begin(0, 0)
+        turn_new(a7)
+        y_begin(0, 1)
+        y_begin(0, 2)
+        scale_new(a7)
+        cand_tanh(b7)
+        state_new(b6, VE)
+        y_begin(0, 3)
+        q1a = turn_q(1, 0)
+        save_new(a6, SC)
+        lay_q(1, 0, q1a, SC)
+        state_diff(b7)
+        turn_new(b6)
+        quant_q(1, 0)
+        state_gate(b7, VE)
+        save_new(a7, SC)
+        scale_new(b6)
+        state_new(b7, VE)
+        save_new(b6, SC)
+        y_end(0, 0)
+        y_end(0, 1)
+        turn_new(b7)
+        scale_new(b7)
+        save_new(b7, SC)
+        y_end(0, 2)
+        y_end(0, 3)
+        y_evac(0, 0)
+        store_new(512, 0, 4)
+        store_new(768, 0, 4)
+        y_evac(0, 1)
+        y_end(1, 0)
+        q1b = turn_q(1, 1)
+        y_evac(0, 2)
+        lay_q(1, 1, q1b, SC)
+        y_end(1, 1)
+        y_evac(0, 3)
+        quant_q(1, 1)
+        y_end(1, 2)
+        y_evac(1, 0)
+        y_end(1, 3)
+        y_evac(1, 1)
+        for m in (2, 3):
+            for v in range(4):
+                y_end(m, v)
+                y_evac(m if v >= 2 else m - 1, (v + 2) % 4)
+        y_evac(3, 2)
+        y_evac(3, 3)

@@ -28,7 +28,7 @@ def tile_gru_candidate_projection_f7_kernel(
     nc = tc.nc
     with ExitStack() as ctx:
         keep = ctx.enter_context(tc.tile_pool(name="keep", bufs=1))
-        work = ctx.enter_context(tc.tile_pool(name="work", bufs=3))
+        work = ctx.enter_context(tc.tile_pool(name="work", bufs=5))
         ypool = ctx.enter_context(tc.tile_pool(name="ypool", bufs=3))
         psum = ctx.enter_context(tc.psum_pool(name="psum", bufs=8))
         ctx.enter_context(tc.manual_schedule())
@@ -63,32 +63,32 @@ def tile_gru_candidate_projection_f7_kernel(
         nc.vector.memset(osc[:].rearrange("p g n -> p (g n)").bitcast(I32), 0)
         make_identity(nc, ident[:])
         nc.gpsimd.tensor_copy(out=ident_bf[:], in_=ident[:])
-        nc.gpsimd.dma_start(out=rows[0:24, :], in_=bias.rearrange("(r c) -> r c", c=P))
-        nc.gpsimd.dma_start(out=rows[24:32, :], in_=bias_c.rearrange("(r c) -> r c", c=P))
-        nc.gpsimd.dma_start(out=rows[32:40, :], in_=carry.rearrange("(r c) -> r c", c=P))
 
-        nc.scalar.dma_start(out=xs[:], in_=x_scale.rearrange("o k -> (o k)").partition_broadcast(P))
-        nc.scalar.activation(out=junk[:], in_=junk[:], func=ACT.Sigmoid)
-
-        def load_wu(dst, lo, hi):
-            for g in range(3):
+        h_view = h.rearrange("(m p) d -> p m d", p=P)
+        def load_wu(dst, lo, hi, gs):
+            for g in gs:
                 src = u_words[g] if g < 2 else w_words[0]
                 nc.sync.dma_start(out=dst[:, g, :, :], in_=src.rearrange("p (s n) -> p s n", s=3)[:, :, lo:hi])
 
-        h_view = h.rearrange("(m p) d -> p m d", p=P)
         nc.sync.dma_start(out=hsb[:, 0, :], in_=h_view[:, 0, :])
+        nc.scalar.dma_start(out=xs[:], in_=x_scale.rearrange("o k -> (o k)").partition_broadcast(P))
         nc.sync.dma_start(out=xb[:], in_=x_bytes.rearrange("(m p) d -> p m d", p=P))
         nc.sync.dma_start(out=hsb[:, 1, :], in_=h_view[:, 1, :])
-        load_wu(wuA, 0, 512)
         for q in range(4):
             nc.sync.dma_start(
                 out=us[32 * q : 32 * q + 4, :, :].bitcast(I32),
                 in_=u_scales[:, 4 * q : 4 * q + 4, :].rearrange("g q n -> q g n").bitcast(I32),
             )
+        load_wu(wuA, 0, 512, (0, 1, 2))
+        nc.scalar.activation(out=junk[:], in_=junk[:], func=ACT.Sigmoid)
         for q in range(4):
             nc.sync.dma_start(out=ws[32 * q : 32 * q + 4, :].bitcast(I32), in_=w_scales[0, 4 * q : 4 * q + 4, :].bitcast(I32))
-        nc.sync.dma_start(out=hsb[:, 2:4, :], in_=h_view[:, 2:4, :])
-        load_wu(wuB, 512, 2048)
+        nc.gpsimd.dma_start(out=hsb[:, 2:4, :], in_=h_view[:, 2:4, :])
+        nc.gpsimd.dma_start(out=rows[0:24, :], in_=bias.rearrange("(r c) -> r c", c=P))
+        nc.gpsimd.dma_start(out=rows[24:32, :], in_=bias_c.rearrange("(r c) -> r c", c=P))
+        nc.gpsimd.dma_start(out=rows[32:40, :], in_=carry.rearrange("(r c) -> r c", c=P))
+
+        load_wu(wuB, 512, 2048, (0, 1, 2))
         nc.sync.dma_start(out=gain_b[:], in_=gain.partition_broadcast(P))
         nc.sync.dma_start(out=bo_b[:], in_=bias_o.partition_broadcast(P))
         for q in range(4):
@@ -224,16 +224,20 @@ def tile_gru_candidate_projection_f7_kernel(
         def cand_tanh(u):
             nc.scalar.activation(out=u["cand"], in_=u["t2"], func=ACT.Tanh, bias=bias_col(2, u["j"]))
 
-        def turn_state(u):
+        HT = {}
+
+        def turn_h_state(j, m0, nm):
             t = bank(BF16)
-            j = u["j"]
-            for k in range(u["nm"]):
-                nc.tensor.transpose(t[:, k * P : (k + 1) * P], hsb[:, u["m0"] + k, j * P : (j + 1) * P], ident_bf[:])
-            u["hT"] = t[:, 0 : u["n"]]
+            for k in range(nm):
+                nc.tensor.transpose(t[:, k * P : (k + 1) * P], hsb[:, m0 + k, j * P : (j + 1) * P], ident_bf[:])
+            HT[j, m0] = t[:, 0 : nm * P]
+
+        def turn_state(u):
+            turn_h_state(u["j"], u["m0"], u["nm"])
 
         def state_diff(u):
             nc.vector.scalar_tensor_tensor(
-                out=u["d"], in0=u["hT"], scalar=bias_col(PART_CARRY, u["j"]), in1=u["cand"], op0=ALU.mult, op1=ALU.subtract
+                out=u["d"], in0=HT[u["j"], u["m0"]], scalar=bias_col(PART_CARRY, u["j"]), in1=u["cand"], op0=ALU.mult, op1=ALU.subtract
             )
 
         def state_gate(u, eng):
@@ -302,202 +306,218 @@ def tile_gru_candidate_projection_f7_kernel(
             nc.sync.dma_start(out=y_out[:, m, ps], in_=ys[:, ps])
 
         G, VE, SC, VC = nc.gpsimd, nc.vector, nc.scalar.copy, nc.vector.tensor_copy
+        t_h0 = turn_h(0)
+        lay_h(0, t_h0, SC)
         scale_x(0)
         scale_x(1)
-        t_h0 = turn_h(0)
-        t_x0 = turn_x(0)
-        t_h1 = turn_h(1)
-        lay_h(0, t_h0, SC)
-        lay_x(0, t_x0, VC)
-        lay_h(1, t_h1, SC)
         quant_h(0)
-        quant_x(0)
+        t_h1 = turn_h(1)
+        t_x0 = turn_x(0)
+        lay_h(1, t_h1, SC)
         scale_x(2)
-        quant_h(1)
+        lay_x(0, t_x0, SC)
         scale_x(3)
+        quant_h(1)
+        quant_x(0)
+        u0 = start_unit(0, 0, 4)
+        FIRST = [("ch",), ("r",), ("cx",), ("z",)]
+        mm_tiles(u0, FIRST[:1], (0, 1))
+        t_x1 = turn_x(1)
+        lay_x(1, t_x1, VC)
+        mm_tiles(u0, FIRST[1:], (0,))
         t_h2 = turn_h(2)
         t_h3 = turn_h(3)
         lay_h(2, t_h2, SC)
+        quant_x(1)
         lay_h(3, t_h3, VC)
-        t_x1 = turn_x(1)
+        mm_tiles(u0, FIRST[1:], (1,))
         rows_t = bank(BF16)
         nc.tensor.transpose(rows_t[:, 0:P], rows[:], ident_bf[:])
-        lay_x(1, t_x1, SC)
         quant_h(2)
         quant_h(3)
         nc.scalar.copy(out=cols[:], in_=rows_t[:, 0:P])
-        quant_x(1)
-        u0 = start_unit(0, 0, 4)
-        FIRST = [("r",), ("ch",), ("cx",), ("z",)]
-        mm_tiles(u0, FIRST, (0, 1))
         turn_state(u0)
         mm_tiles(u0, FIRST, (2, 3))
-        sig(u0, "r", 0)
-        cand_in(u0)
-        cand_sum(u0)
-        sig(u0, "z", 1)
 
-        U = {0: u0}
-        for j in range(1, 6):
-            u = start_unit(j, 0, 4)
-            p = U[j - 1]
-            U[j] = u
-            mm_full(u, ("r", "ch", "cx"))
-            cand_tanh(p)
-            state_diff(p)
-            state_gate(p, G)
-            state_new(p, G)
-            sig(u, "r", 0)
-            cand_in(u)
-            cand_sum(u)
-            if j >= 3:
-                turn_new(U[j - 3])
-            turn_state(u)
-            mm_full(u, ("z",))
-            if j >= 3:
-                save_new(U[j - 3], SC)
-                scale_new(U[j - 3])
-            sig(u, "z", 1)
-            if j == 5:
-                store_new(0, 0, 4)
+        NF = 5
+        ops = []
+        where = {}
 
-        PAIR = [("r", "ch"), ("cx", "z")]
-        def mm1(u):
-            mm_tiles(u, PAIR[:1], (u["m0"], u["m0"] + 1))
-        def mm2(u):
-            mm_tiles(u, PAIR[1:], (u["m0"], u["m0"] + 1))
-        a6, a7, b6, b7 = start_unit(6, 0, 2), start_unit(7, 0, 2), start_unit(6, 2, 2), start_unit(7, 2, 2)
-        p5 = U[5]
-        mm1(a6)
-        cand_tanh(p5)
-        state_diff(p5)
-        state_gate(p5, G)
-        state_new(p5, G)
-        turn_new(U[3])
-        turn_state(a6)
-        mm2(a6)
-        save_new(U[3], SC)
-        scale_new(U[3])
-        sig(a6, "r", 0)
-        mm1(a7)
-        sig(a6, "z", 1)
-        cand_in(a6)
-        turn_new(U[4])
-        turn_state(a7)
-        mm2(a7)
-        save_new(U[4], SC)
-        cand_sum(a6)
-        sig(a7, "r", 0)
-        scale_new(U[4])
-        store_new(256, 0, 4)
-        mm1(b6)
-        cand_tanh(a6)
-        cand_in(a7)
-        sig(a7, "z", 1)
-        q0a = turn_q(0, 0)
-        q0b = turn_q(0, 1)
-        turn_state(b6)
-        mm2(b6)
-        state_diff(a6)
-        cand_sum(a7)
-        lay_q(0, 0, q0a, SC)
-        state_gate(a6, VE)
-        sig(b6, "r", 0)
-        lay_q(0, 1, q0b, VC)
-        state_new(a6, G)
-        mm1(b7)
-        cand_tanh(a7)
-        cand_in(b6)
-        sig(b6, "z", 1)
-        turn_new(p5)
-        turn_state(b7)
-        mm2(b7)
-        state_diff(a7)
-        cand_sum(b6)
-        save_new(p5, SC)
-        state_gate(a7, VE)
-        sig(b7, "r", 0)
-        quant_q(0, 0)
-        scale_new(p5)
-        state_new(a7, G)
-        quant_q(0, 1)
-        cand_tanh(b6)
-        turn_new(a6)
-        cand_in(b7)
-        sig(b7, "z", 1)
-        state_diff(b6)
-        cand_sum(b7)
-        scale_new(a6)
-        state_gate(b6, VE)
+        def op(eng, cost, fn, args, needs, opens=0, closes=0, name=None):
+            where[name or (fn, args)] = len(ops)
+            ops.append((eng, cost, fn, args, [where[x] for x in needs], opens, closes))
+
+        live = {(0, 0, MT): u0}
         ys = {}
-        BY_SCALAR = ((0, 2), (1, 0), (1, 2), (2, 0), (2, 2), (3, 0))
         banks = {}
-        def y_begin(m, v):
-            t = bank()
-            banks[m, v] = t
-            y_mm(m, v, (0,), t)
-        def y_end(m, v):
-            if (m, v) not in banks:
-                y_begin(m, v)
-            y_mm(m, v, (1,), banks[m, v])
-        def y_evac(m, v):
-            if v == 0:
+        qbanks = {}
+        PAIRS = (("r", "ch"), ("cx", "z"))
+
+        def begin(key):
+            if key not in live:
+                live[key] = start_unit(*key)
+            return live[key]
+
+        def mm_op(key, names):
+            u = begin(key)
+            if key[2] == MT:
+                mm_full(u, names)
+            else:
+                mm_tiles(u, [names], (key[1], key[1] + 1))
+
+        def sig_op(key, name, s):
+            sig(live[key], name, s)
+
+        def do(fn, key, *args):
+            fn(live[key], *args)
+
+        def turn_q_op(g, mp):
+            qbanks[g, mp] = turn_q(g, mp)
+
+        def lay_q_op(g, mp, copy):
+            lay_q(g, mp, qbanks[g, mp], copy)
+
+        def y_op(m, v, g):
+            if g == 0:
+                banks[m, v] = bank()
+            y_mm(m, v, (g,), banks[m, v])
+
+        def y_tile(m):
+            if m not in ys:
                 yt = ypool.tile([P, V], F32, name="ys")
                 ys[m] = yt
-            if (m, v) in BY_SCALAR:
-                vs = slice(v * 512, (v + 1) * 512)
-                nc.scalar.copy(out=ys[m][:, vs], in_=banks[m, v][:])
-                nc.gpsimd.tensor_tensor(out=ys[m][:, vs], in0=ys[m][:, vs], in1=bo_b[:, vs], op=ALU.add)
-            else:
-                y_add(m, v, banks[m, v], ys[m])
-            if m == 3 and v >= 2:
-                y_store(m, v, 1, ys[m])
-            elif v % 2 == 1:
-                y_store(m, v - 1, 2, ys[m])
-        y_begin(0, 0)
-        turn_new(a7)
-        y_begin(0, 1)
-        y_begin(0, 2)
-        scale_new(a7)
-        cand_tanh(b7)
-        state_new(b6, VE)
-        y_begin(0, 3)
-        q1a = turn_q(1, 0)
-        save_new(a6, SC)
-        lay_q(1, 0, q1a, SC)
-        state_diff(b7)
-        turn_new(b6)
-        quant_q(1, 0)
-        state_gate(b7, VE)
-        save_new(a7, SC)
-        scale_new(b6)
-        state_new(b7, VE)
-        save_new(b6, SC)
-        y_end(0, 0)
-        y_end(0, 1)
-        turn_new(b7)
-        scale_new(b7)
-        save_new(b7, SC)
-        y_end(0, 2)
-        y_end(0, 3)
-        y_evac(0, 0)
-        store_new(512, 0, 4)
-        store_new(768, 0, 4)
-        y_evac(0, 1)
-        y_end(1, 0)
-        q1b = turn_q(1, 1)
-        y_evac(0, 2)
-        lay_q(1, 1, q1b, SC)
-        y_end(1, 1)
-        y_evac(0, 3)
-        quant_q(1, 1)
-        y_end(1, 2)
-        y_evac(1, 0)
-        y_end(1, 3)
-        y_evac(1, 1)
-        for m in (2, 3):
+            return ys[m]
+
+        def y_add_op(m, v):
+            y_add(m, v, banks[m, v], y_tile(m))
+
+        def y_copy_op(m, v):
+            nc.scalar.copy(out=y_tile(m)[:, v * 512 : (v + 1) * 512], in_=banks[m, v][:])
+
+        def y_bias_op(m, v):
+            vs = slice(v * 512, (v + 1) * 512)
+            nc.gpsimd.tensor_tensor(out=ys[m][:, vs], in0=ys[m][:, vs], in1=bo_b[:, vs], op=ALU.add)
+
+        def y_store_op(m, v, n):
+            y_store(m, v, n, ys[m])
+
+        units = [(j, 0, MT) for j in range(NF)] + [(j, m0, 2) for m0 in (0, 2) for j in range(NF, JT)]
+        pend_turn = []
+
+        def q_ops(g, mp):
+            js = range(4 * g, 4 * g + 4)
+            needs = [("q", (j, 0, MT) if j < NF else (j, 2 * mp, 2)) for j in js]
+            op("pe", 4 * 128, turn_q_op, (g, mp), needs, opens=1, name=("turn_q", g, mp))
+            op("act", 540, lay_q_op, (g, mp, SC), [("turn_q", g, mp)], closes=1, name=("lay_q", g, mp))
+            op("dve", 290, quant_q, (g, mp), [("lay_q", g, mp)], name=("qq", g, mp))
+
+        def tail_ops(key):
+            j, m0, nm = key
+            n = nm * P
+            for fn, nm_, need, on_v in ((state_gate, "e", [("d", key), ("z", key)], m0 == 2 and j >= 5), (state_new, "new", [("e", key)], m0 == 2 and j >= 5)):
+                eng, name, cost = (VE, "dve", n + 40) if on_v else (G, "pool", 2.4 * n + 40)
+                op(name, cost, do, (fn, key, eng), need, name=(nm_, key))
+            op("pe", 104 * nm, do, (turn_new, key), [("new", key)], opens=1, name=("turn_new", key))
+            op("act", n + 40, do, (save_new, key, SC), [("turn_new", key)], name=("save", key))
+            op("dve", n + 40, do, (scale_new, key), [("turn_new", key), ("save", key)], closes=1, name=("q", key))
+            if nm == MT and j % 2 == 1:
+                op("sp", 90, store_new, ((j - 1) * P, 0, MT), [("save", key), ("save", (j - 1, 0, MT))], name=("st", key))
+            if nm == 2 and j % 2 == 1:
+                other = (j - 1, 0, MT) if j - 1 < NF else (j - 1, m0, 2)
+                op("sp", 90, store_new, ((j - 1) * P, m0, 2), [("save", key), ("save", other)], name=("st", key))
+
+        def y_ops(m):
+            mp = m // 2
             for v in range(4):
-                y_end(m, v)
-                y_evac(m if v >= 2 else m - 1, (v + 2) % 4)
-        y_evac(3, 2)
-        y_evac(3, 3)
+                op("pe", 262, y_op, (m, v, 0), [("qq", 0, mp)], opens=1, name=("y0", m, v))
+            for v in range(4):
+                op("pe", 262, y_op, (m, v, 1), [("qq", 1, mp), ("y0", m, v)], name=("y1", m, v))
+                if v == 1:
+                    op("act", 545, y_copy_op, (m, v), [("y1", m, v)], closes=1, name=("yc", m, v))
+                    op("pool", 1270, y_bias_op, (m, v), [("yc", m, v)], name=("ya", m, v))
+                else:
+                    op("dve", 555, y_add_op, (m, v), [("y1", m, v)], closes=1, name=("ya", m, v))
+            for v in range(0, 4, 1):
+                op("sp", 90, y_store_op, (m, v, 1), [("ya", m, x) for x in range(v, v + 1)], name=("ys", m, v))
+
+        chains = []
+        for key in units:
+            j, m0, nm = key
+            n = nm * P
+            half = nm == 2
+            k = 78 * 2 if half else 262
+            if j > 0:
+                if half:
+                    op("pe", 5 * k, mm_op, (key, ("r", "ch")), [], opens=1, name=("rch", key))
+                    op("pe", 4 * k, mm_op, (key, ("cx", "z")), [], opens=1, name=("cxz", key))
+                    where["r", key] = where["ch", key] = where["rch", key]
+                    where["cx", key] = where["zz", key] = where["cxz", key]
+                else:
+                    op("pe", 3 * k, mm_op, (key, ("r",)), [], opens=1, name=("r", key))
+                    op("pe", 2 * k, mm_op, (key, ("ch",)), [], opens=1, name=("ch", key))
+                    op("pe", k, mm_op, (key, ("cx",)), [], opens=1, name=("cx", key))
+                    op("pe", 3 * k, mm_op, (key, ("z",)), [], opens=1, name=("zz", key))
+                op("pe", 64 * nm, turn_h_state, key, [], opens=1, name=("hT", key))
+            else:
+                op("pe", 1, len, ((),), [], opens=5, name=("r", key))
+                for x in ("ch", "cx", "zz", "hT"):
+                    where[x, key] = where["r", key]
+            op("act", n + 40, sig_op, (key, "r", 0), [("r", key)], closes=0 if half else 1, name=("sr", key))
+            op("dve", n + 45, do, (cand_in, key), [("sr", key), ("ch", key)], closes=1, name=("t1", key))
+            op("dve", n + 45, do, (cand_sum, key), [("t1", key), ("cx", key)], closes=0 if half else 1, name=("t2", key))
+            op("act", n + 40, do, (cand_tanh, key), [("t2", key)], name=("cand", key))
+            op("act", n + 40, sig_op, (key, "z", 1), [("zz", key)] + ([("t2", key)] if half else []), closes=1, name=("z", key))
+            op("dve", n + 45, do, (state_diff, key), [("cand", key), ("hT", key)], closes=1, name=("d", key))
+            tail_ops(key)
+            if key == (3, 0, MT):
+                q_ops(0, 0)
+                q_ops(0, 1)
+            if j == 3 and half:
+                q_ops(0, m0 // 2)
+            if j == JT - 1:
+                q_ops(1, m0 // 2)
+        for m in range(MT):
+            y_ops(m)
+
+        free = {}
+        end = [None] * len(ops)
+        kinds = [o[0] for o in ops]
+        pending = {e: [i for i in range(len(ops)) if kinds[i] == e] for e in ("pe", "act", "dve", "pool", "sp")}
+        used, release = 0, []
+        order = []
+        while any(pending.values()):
+            best = None
+            for e, queue in pending.items():
+                t0 = free.get(e, 0)
+                pick = None
+                for i in queue[:60]:
+                    o = ops[i]
+                    if any(end[x] is None for x in o[4]):
+                        continue
+                    t = max([t0] + [end[x] + (0 if kinds[x] == e == "pe" else 460 if kinds[x] == "pe" else 250) for x in o[4]])
+                    spare = 8 - used
+                    if o[5] > spare:
+                        short = o[5] - spare
+                        if short > len(release):
+                            continue
+                        t = max(t, sorted(release)[short - 1] + 250)
+                    if pick is None or t < pick[0]:
+                        pick = (t, i)
+                    if t == t0:
+                        break
+                if pick and (best is None or pick[0] < best[0]):
+                    best = pick + (e,)
+            t, i, e = best
+            o = ops[i]
+            pending[e].remove(i)
+            order.append(i)
+            if o[5]:
+                spare = 8 - used
+                short = max(0, o[5] - spare)
+                release = sorted(release)[short:]
+                used += o[5] - short
+            free[e] = t + o[1]
+            end[i] = t + o[1]
+            release += [end[i] + 250] * o[6]
+        for i in order:
+            ops[i][2](*ops[i][3])

@@ -41,8 +41,9 @@ def tile_gru_candidate_projection_f7_kernel(
         ident = keep.tile([P, P], F32, name="ident")
         ident_bf = keep.tile([P, P], BF16, name="ident_bf")
         rows = keep.tile([P, P], BF16, name="rows")
-        cols = keep.tile([P, P], F32, name="cols")
-        xs = keep.tile([P, D], F32, name="xs")
+        cols = keep.tile([P, 48], F32, name="cols")
+        gain_c = keep.tile([P, JT], BF16, name="gain_c")
+        xs4 = keep.tile([P, 4], F32, name="xs4")
         xb = keep.tile([P, MT, D], U8, name="xb", align_bytes=64)
         xf = keep.tile([P, MT, D], BF16, name="xf", align_bytes=64)
         hsb = keep.tile([P, MT, H], BF16, name="hsb", align_bytes=64)
@@ -55,14 +56,21 @@ def tile_gru_candidate_projection_f7_kernel(
         gain_b = keep.tile([P, H], BF16, name="gain_b")
         bo_b = keep.tile([P, V], BF16, name="bo_b")
         junk = keep.tile([P, 1], F32, name="junk")
+        warm = keep.tile([P, 512], BF16, name="warm")
 
+        nc.vector.memset(junk[:], 0.0)
+        nc.vector.memset(warm[:], 0.0)
+        nc.vector.memset(rows[:], 0.0)
         nc.vector.memset(us[:].rearrange("p g n -> p (g n)").bitcast(I32), 0)
         nc.vector.memset(ws[:].bitcast(I32), 0)
-        nc.vector.memset(rows[:], 0.0)
-        nc.vector.memset(junk[:], 0.0)
         nc.vector.memset(osc[:].rearrange("p g n -> p (g n)").bitcast(I32), 0)
         make_identity(nc, ident[:])
         nc.gpsimd.tensor_copy(out=ident_bf[:], in_=ident[:])
+        first_row = 0
+        for vec in (gain, bias, bias_c, carry):
+            n = vec.shape[0] // P
+            nc.gpsimd.dma_start(out=rows[first_row : first_row + n, :], in_=vec.rearrange("(r c) -> r c", c=P))
+            first_row += n
 
         h_view = h.rearrange("(m p) d -> p m d", p=P)
         def load_wu(dst, lo, hi, gs):
@@ -71,45 +79,38 @@ def tile_gru_candidate_projection_f7_kernel(
                 nc.sync.dma_start(out=dst[:, g, :, :], in_=src.rearrange("p (s n) -> p s n", s=3)[:, :, lo:hi])
 
         nc.sync.dma_start(out=hsb[:, 0, :], in_=h_view[:, 0, :])
-        nc.scalar.dma_start(out=xs[:], in_=x_scale.rearrange("o k -> (o k)").partition_broadcast(P))
         nc.sync.dma_start(out=xb[:], in_=x_bytes.rearrange("(m p) d -> p m d", p=P))
         nc.sync.dma_start(out=hsb[:, 1, :], in_=h_view[:, 1, :])
-        for q in range(4):
-            nc.sync.dma_start(
-                out=us[32 * q : 32 * q + 4, :, :].bitcast(I32),
-                in_=u_scales[:, 4 * q : 4 * q + 4, :].rearrange("g q n -> q g n").bitcast(I32),
-            )
-        load_wu(wuA, 0, 512, (0, 1, 2))
+        nc.scalar.dma_start(out=xs4[:], in_=x_scale.rearrange("o (p t) -> p (o t)", t=4))
         nc.scalar.activation(out=junk[:], in_=junk[:], func=ACT.Sigmoid)
-        for q in range(4):
-            nc.sync.dma_start(out=ws[32 * q : 32 * q + 4, :].bitcast(I32), in_=w_scales[0, 4 * q : 4 * q + 4, :].bitcast(I32))
-        nc.gpsimd.dma_start(out=hsb[:, 2:4, :], in_=h_view[:, 2:4, :])
-        nc.gpsimd.dma_start(out=rows[0:24, :], in_=bias.rearrange("(r c) -> r c", c=P))
-        nc.gpsimd.dma_start(out=rows[24:32, :], in_=bias_c.rearrange("(r c) -> r c", c=P))
-        nc.gpsimd.dma_start(out=rows[32:40, :], in_=carry.rearrange("(r c) -> r c", c=P))
-
+        for r in range(4):
+            nc.sync.dma_start(out=us[r:P:32, :, :].bitcast(I32), in_=u_scales.rearrange("g (b r) n -> r b g n", r=4)[r].bitcast(I32))
+        load_wu(wuA, 0, 512, (0, 1, 2))
+        nc.sync.dma_start(out=hsb[:, 2:4, :], in_=h_view[:, 2:4, :])
+        for r in range(4):
+            nc.sync.dma_start(out=ws[r:P:32, :].bitcast(I32), in_=w_scales.rearrange("g (b r) n -> r b (g n)", r=4)[r].bitcast(I32))
         load_wu(wuB, 512, 2048, (0, 1, 2))
-        nc.sync.dma_start(out=gain_b[:], in_=gain.partition_broadcast(P))
-        nc.sync.dma_start(out=bo_b[:], in_=bias_o.partition_broadcast(P))
-        for q in range(4):
-            nc.sync.dma_start(
-                out=osc[32 * q : 32 * q + 4, :, :].bitcast(I32),
-                in_=o_scales[:, 4 * q : 4 * q + 4, :].rearrange("g q n -> q g n").bitcast(I32),
-            )
+        for r in range(4):
+            nc.sync.dma_start(out=osc[r:P:32, :, :].bitcast(I32), in_=o_scales.rearrange("g (b r) n -> r b g n", r=4)[r].bitcast(I32))
         for g in range(2):
             for half in range(2):
                 ps = slice(4096 * half, 4096 * half + 4096)
                 nc.sync.dma_start(out=ow[:, g, ps].bitcast(I32), in_=o_words[g].rearrange("p n t -> p (n t)")[:, ps].bitcast(I32))
+        nc.sync.dma_start(out=bo_b[:], in_=bias_o.partition_broadcast(P))
 
         hin = keep.tile([P, 2, B, 4], BF16, name="hin", align_bytes=64)
         xin = keep.tile([P, B, 4], BF16, name="xin", align_bytes=64)
         hxc = keep.tile([P, 3, B], U32, name="hxc", align_bytes=256)
         hxs = keep.tile([P, 3, B], U8, name="hxs", align_bytes=256)
         hin_words = hin[:].rearrange("p g r t -> p g (r t)").bitcast(F32)
-        xin_words = xin[:].rearrange("p r t -> p (r t)").bitcast(F32)
 
-        def scale_x(m):
-            nc.vector.tensor_tensor(out=xf[:, m, :], in0=xb[:, m, :].bitcast(FP8), in1=xs[:], op=ALU.mult)
+        def widen_x(m, copy):
+            copy(out=xf[:, m, :], in_=xb[:, m, :].bitcast(FP8))
+
+        def dummy(n):
+            t = bank()
+            for i in range(n):
+                nc.tensor.matmul(t[:], lhsT=warm[:, 0:P], rhs=warm[:], start=True, stop=True)
 
         def turn_h(m):
             words = hsb[:, m, :].bitcast(F32)
@@ -133,9 +134,16 @@ def tile_gru_candidate_projection_f7_kernel(
             dst = hin_words[:, :, m * 256 : (m + 1) * 256].rearrange("p g (r u) -> p g r u", u=2)
             copy(out=dst, in_=t[:].rearrange("p (g u r) -> p g r u", g=2, u=2))
 
-        def lay_x(mp, t, copy):
-            dst = xin_words[:, mp * 512 : (mp + 1) * 512].rearrange("p (m r u) -> p m r u", m=2, u=2)
-            copy(out=dst, in_=t[:].rearrange("p (m u r) -> p m r u", m=2, u=2))
+        def lay_x(mp, t):
+            scales = xs4[:].rearrange("p (u e) -> p u e", e=2).unsqueeze(1).to_broadcast([P, P, 2, 2])
+            for mm in range(2):
+                m = 2 * mp + mm
+                nc.vector.tensor_tensor(
+                    out=xin[:, m * P : (m + 1) * P, :].rearrange("p r (u e) -> p r u e", e=2),
+                    in0=t[:, 256 * mm : 256 * (mm + 1)].bitcast(BF16).rearrange("p (u r e) -> p r u e", u=2, e=2),
+                    in1=scales,
+                    op=ALU.mult,
+                )
 
         def quant_h(m):
             rs = slice(m * P, (m + 1) * P)
@@ -148,7 +156,7 @@ def tile_gru_candidate_projection_f7_kernel(
             rs = slice(mp * 256, (mp + 1) * 256)
             nc.vector.quantize_mx(out=hxc[:, 2, rs].bitcast(E4M3X4), scales=hxs[:, 2, rs], in_=xin[:, rs, :].rearrange("p r t -> p (r t)"))
 
-        bias_col = lambda part, j: cols[:, part * JT + j : part * JT + j + 1]
+        bias_col = lambda part, j: cols[:, (part + 1) * JT + j : (part + 1) * JT + j + 1]
         PART_BC, PART_CARRY = 3, 4
 
         def wu_slice(g, s, j):
@@ -306,40 +314,49 @@ def tile_gru_candidate_projection_f7_kernel(
             nc.sync.dma_start(out=y_out[:, m, ps], in_=ys[:, ps])
 
         G, VE, SC, VC = nc.gpsimd, nc.vector, nc.scalar.copy, nc.vector.tensor_copy
+        dummy(4)
         t_h0 = turn_h(0)
         lay_h(0, t_h0, SC)
-        scale_x(0)
-        scale_x(1)
-        quant_h(0)
-        t_h1 = turn_h(1)
+        widen_x(0, VC)
+        widen_x(1, VC)
+        widen_x(2, VC)
+        widen_x(3, VC)
+        dummy(1)
         t_x0 = turn_x(0)
+        t_x1 = turn_x(1)
+        t_h1 = turn_h(1)
+        quant_h(0)
+        lay_x(0, t_x0)
         lay_h(1, t_h1, SC)
-        scale_x(2)
-        lay_x(0, t_x0, SC)
-        scale_x(3)
-        quant_h(1)
         quant_x(0)
+        quant_h(1)
+        lay_x(1, t_x1)
         u0 = start_unit(0, 0, 4)
         FIRST = [("ch",), ("r",), ("cx",), ("z",)]
-        mm_tiles(u0, FIRST[:1], (0, 1))
-        t_x1 = turn_x(1)
-        lay_x(1, t_x1, VC)
-        mm_tiles(u0, FIRST[1:], (0,))
+        dummy(2)
+        mm_tiles(u0, FIRST, (0, 1))
         t_h2 = turn_h(2)
         t_h3 = turn_h(3)
         lay_h(2, t_h2, SC)
         quant_x(1)
         lay_h(3, t_h3, VC)
-        mm_tiles(u0, FIRST[1:], (1,))
         rows_t = bank(BF16)
         nc.tensor.transpose(rows_t[:, 0:P], rows[:], ident_bf[:])
+        nc.scalar.copy(out=gain_c[:], in_=rows_t[:, 0:JT])
+        nc.scalar.copy(out=cols[:], in_=rows_t[:, 0:48])
+        gain_t = [bank(), bank()]
+        for j in range(JT):
+            nc.tensor.matmul(
+                gain_t[j // 4][:, j % 4 * P : (j % 4 + 1) * P], lhsT=gain_c[:, j : j + 1].to_broadcast([P, P]), rhs=ident_bf[:], start=True, stop=True
+            )
         quant_h(2)
         quant_h(3)
-        nc.scalar.copy(out=cols[:], in_=rows_t[:, 0:P])
         turn_state(u0)
         mm_tiles(u0, FIRST, (2, 3))
+        for c in range(2):
+            nc.scalar.copy(out=gain_b[:, c * 512 : (c + 1) * 512], in_=gain_t[c][:])
 
-        NF = 5
+        NF = 6
         ops = []
         where = {}
 
@@ -417,7 +434,10 @@ def tile_gru_candidate_projection_f7_kernel(
             for fn, nm_, need, on_v in ((state_gate, "e", [("d", key), ("z", key)], m0 == 2 and j >= 5), (state_new, "new", [("e", key)], m0 == 2 and j >= 5)):
                 eng, name, cost = (VE, "dve", n + 40) if on_v else (G, "pool", 2.4 * n + 40)
                 op(name, cost, do, (fn, key, eng), need, name=(nm_, key))
-            op("pe", 104 * nm, do, (turn_new, key), [("new", key)], opens=1, name=("turn_new", key))
+
+        def after_turn(key):
+            j, m0, nm = key
+            n = nm * P
             op("act", n + 40, do, (save_new, key, SC), [("turn_new", key)], name=("save", key))
             op("dve", n + 40, do, (scale_new, key), [("turn_new", key), ("save", key)], closes=1, name=("q", key))
             if nm == MT and j % 2 == 1:
@@ -425,6 +445,13 @@ def tile_gru_candidate_projection_f7_kernel(
             if nm == 2 and j % 2 == 1:
                 other = (j - 1, 0, MT) if j - 1 < NF else (j - 1, m0, 2)
                 op("sp", 90, store_new, ((j - 1) * P, m0, 2), [("save", key), ("save", other)], name=("st", key))
+            if key == (3, 0, MT):
+                q_ops(0, 0)
+                q_ops(0, 1)
+            if j == 3 and nm == 2:
+                q_ops(0, m0 // 2)
+            if j == JT - 1:
+                q_ops(1, m0 // 2)
 
         def y_ops(m):
             mp = m // 2
@@ -440,24 +467,37 @@ def tile_gru_candidate_projection_f7_kernel(
             for v in range(0, 4, 1):
                 op("sp", 90, y_store_op, (m, v, 1), [("ya", m, x) for x in range(v, v + 1)], name=("ys", m, v))
 
-        chains = []
-        for key in units:
+        def run_op(key, others):
+            turn_h_state(*key)
+            for other in others:
+                turn_new(live[other])
+
+        with_run = {}
+        for at, key in enumerate(units):
+            k = at + (3 if key[2] == MT else 5)
+            with_run.setdefault(units[k] if k < len(units) else None, []).append(key)
+        for at, key in enumerate(units):
             j, m0, nm = key
             n = nm * P
             half = nm == 2
             k = 78 * 2 if half else 262
+            room = [("d", units[at - 3])] if at >= 3 else []
             if j > 0:
                 if half:
-                    op("pe", 5 * k, mm_op, (key, ("r", "ch")), [], opens=1, name=("rch", key))
+                    op("pe", 5 * k, mm_op, (key, ("r", "ch")), room, opens=1, name=("rch", key))
                     op("pe", 4 * k, mm_op, (key, ("cx", "z")), [], opens=1, name=("cxz", key))
                     where["r", key] = where["ch", key] = where["rch", key]
                     where["cx", key] = where["zz", key] = where["cxz", key]
                 else:
-                    op("pe", 3 * k, mm_op, (key, ("r",)), [], opens=1, name=("r", key))
+                    op("pe", 3 * k, mm_op, (key, ("r",)), room, opens=1, name=("r", key))
                     op("pe", 2 * k, mm_op, (key, ("ch",)), [], opens=1, name=("ch", key))
                     op("pe", k, mm_op, (key, ("cx",)), [], opens=1, name=("cx", key))
                     op("pe", 3 * k, mm_op, (key, ("z",)), [], opens=1, name=("zz", key))
-                op("pe", 64 * nm, turn_h_state, key, [], opens=1, name=("hT", key))
+                others = tuple(with_run.get(key, []))
+                op("pe", 64 * nm + sum(104 * x[2] for x in others), run_op, (key, others), [("new", x) for x in others], opens=1 + len(others), name=("hT", key))
+                for x in others:
+                    where["turn_new", x] = where["hT", key]
+                    after_turn(x)
             else:
                 op("pe", 1, len, ((),), [], opens=5, name=("r", key))
                 for x in ("ch", "cx", "zz", "hT"):
@@ -469,13 +509,9 @@ def tile_gru_candidate_projection_f7_kernel(
             op("act", n + 40, sig_op, (key, "z", 1), [("zz", key)] + ([("t2", key)] if half else []), closes=1, name=("z", key))
             op("dve", n + 45, do, (state_diff, key), [("cand", key), ("hT", key)], closes=1, name=("d", key))
             tail_ops(key)
-            if key == (3, 0, MT):
-                q_ops(0, 0)
-                q_ops(0, 1)
-            if j == 3 and half:
-                q_ops(0, m0 // 2)
-            if j == JT - 1:
-                q_ops(1, m0 // 2)
+        for key in with_run.get(None, []):
+            op("pe", 104 * key[2], do, (turn_new, key), [("new", key)], opens=1, name=("turn_new", key))
+            after_turn(key)
         for m in range(MT):
             y_ops(m)
 

@@ -178,7 +178,7 @@ def tile_gru_candidate_projection_f7_kernel(
                 )
 
         newo = keep.tile([P, MT, H], F32, name="newo")
-        qb = keep.tile([P, MT, H], BF16, name="qb", align_bytes=64)
+        qb = keep.tile([P, MT, 2, 2, P, 2], BF16, name="qb", align_bytes=64)
         qin = keep.tile([P, 2, B, 4], BF16, name="qin", align_bytes=64)
         qc = keep.tile([P, 2, B], U32, name="qc", align_bytes=256)
         qs = keep.tile([P, 2, B], U8, name="qs", align_bytes=256)
@@ -234,14 +234,14 @@ def tile_gru_candidate_projection_f7_kernel(
 
         HT = {}
 
-        def turn_h_state(j, m0, nm):
+        def turn_states(keys):
             t = bank(BF16)
-            for k in range(nm):
-                nc.tensor.transpose(t[:, k * P : (k + 1) * P], hsb[:, m0 + k, j * P : (j + 1) * P], ident_bf[:])
-            HT[j, m0] = t[:, 0 : nm * P]
-
-        def turn_state(u):
-            turn_h_state(u["j"], u["m0"], u["nm"])
+            c = 0
+            for j, m0, nm in keys:
+                HT[j, m0] = t[:, c : c + nm * P]
+                for m in range(m0, m0 + nm):
+                    nc.tensor.transpose(t[:, c : c + P], hsb[:, m, j * P : (j + 1) * P], ident_bf[:])
+                    c += P
 
         def state_diff(u):
             nc.vector.scalar_tensor_tensor(
@@ -261,13 +261,17 @@ def tile_gru_candidate_projection_f7_kernel(
             u["newT"] = t[:, 0 : u["n"]].rearrange("p (m c) -> p m c", c=P)
 
         def scale_new(u):
-            cs = slice(u["j"] * P, (u["j"] + 1) * P)
-            nc.vector.tensor_tensor(
-                out=qb[:, u["m0"] : u["m0"] + u["nm"], cs],
-                in0=u["newT"],
-                in1=gain_b[:, cs].unsqueeze(1).to_broadcast([P, u["nm"], P]),
-                op=ALU.mult,
-            )
+            g, p0 = u["j"] // 4, u["j"] % 4 * 32
+            ms = slice(u["m0"], u["m0"] + u["nm"])
+            by_word = u["newT"].rearrange("p m (k w e) -> p m w k e", w=2, e=2)
+            gain_v = gain_b[:, u["j"] * P : (u["j"] + 1) * P].rearrange("p (k w e) -> p w k e", w=2, e=2)
+            for w in range(2):
+                nc.vector.tensor_tensor(
+                    out=qb[:, ms, g, w, p0 : p0 + 32, :],
+                    in0=by_word[:, :, w, :, :],
+                    in1=gain_v[:, w, :, :].unsqueeze(1).to_broadcast([P, u["nm"], 32, 2]),
+                    op=ALU.mult,
+                )
 
         def save_new(u, copy):
             cs = slice(u["j"] * P, (u["j"] + 1) * P)
@@ -276,10 +280,10 @@ def tile_gru_candidate_projection_f7_kernel(
         def turn_q(g, mp):
             t = bank()
             for mm in range(2):
-                words = qb[:, 2 * mp + mm, :].bitcast(F32)
                 for u in range(2):
                     i = 2 * mm + u
-                    nc.tensor.transpose(t[:, i * P : (i + 1) * P], words[:, 256 * g + u : 256 * (g + 1) : 2], ident[:])
+                    words = qb[:, 2 * mp + mm, g, u, :, :].rearrange("p k e -> p (k e)").bitcast(F32)
+                    nc.tensor.transpose(t[:, i * P : (i + 1) * P], words, ident[:])
             return t
 
         def lay_q(g, mp, t, copy):
@@ -314,6 +318,15 @@ def tile_gru_candidate_projection_f7_kernel(
             nc.sync.dma_start(out=y_out[:, m, ps], in_=ys[:, ps])
 
         G, VE, SC, VC = nc.gpsimd, nc.vector, nc.scalar.copy, nc.vector.tensor_copy
+        state_bank = [bank(BF16), bank(BF16)]
+
+        def head_states(ms):
+            for j in range(4):
+                t = state_bank[j // 2][:, j % 2 * B : (j % 2 + 1) * B]
+                HT[j, 0] = t
+                for m in ms:
+                    nc.tensor.transpose(t[:, m * P : (m + 1) * P], hsb[:, m, j * P : (j + 1) * P], ident_bf[:])
+
         dummy(4)
         t_h0 = turn_h(0)
         lay_h(0, t_h0, SC)
@@ -333,7 +346,7 @@ def tile_gru_candidate_projection_f7_kernel(
         lay_x(1, t_x1)
         u0 = start_unit(0, 0, 4)
         FIRST = [("ch",), ("r",), ("cx",), ("z",)]
-        dummy(2)
+        head_states((0, 1))
         mm_tiles(u0, FIRST, (0, 1))
         t_h2 = turn_h(2)
         t_h3 = turn_h(3)
@@ -351,7 +364,7 @@ def tile_gru_candidate_projection_f7_kernel(
             )
         quant_h(2)
         quant_h(3)
-        turn_state(u0)
+        head_states((2, 3))
         mm_tiles(u0, FIRST, (2, 3))
         for c in range(2):
             nc.scalar.copy(out=gain_b[:, c * 512 : (c + 1) * 512], in_=gain_t[c][:])
@@ -360,23 +373,19 @@ def tile_gru_candidate_projection_f7_kernel(
         ops = []
         where = {}
 
-        def op(eng, cost, fn, args, needs, opens=0, closes=0, name=None):
-            where[name or (fn, args)] = len(ops)
-            ops.append((eng, cost, fn, args, [where[x] for x in needs], opens, closes))
+        def op(eng, cost, fn, args, needs, opens=0, closes=0, name=None, keep=0):
+            where[name] = len(ops)
+            ops.append((eng, cost, fn, args, [where[x] for x in needs], opens, closes, keep))
 
         live = {(0, 0, MT): u0}
         ys = {}
         banks = {}
         qbanks = {}
-        PAIRS = (("r", "ch"), ("cx", "z"))
-
-        def begin(key):
-            if key not in live:
-                live[key] = start_unit(*key)
-            return live[key]
 
         def mm_op(key, names):
-            u = begin(key)
+            if key not in live:
+                live[key] = start_unit(*key)
+            u = live[key]
             if key[2] == MT:
                 mm_full(u, names)
             else:
@@ -388,8 +397,13 @@ def tile_gru_candidate_projection_f7_kernel(
         def do(fn, key, *args):
             fn(live[key], *args)
 
-        def turn_q_op(g, mp):
-            qbanks[g, mp] = turn_q(g, mp)
+        def turns_op(states, news, qs_):
+            if states:
+                turn_states(states)
+            for key in news:
+                turn_new(live[key])
+            for g, mp in qs_:
+                qbanks[g, mp] = turn_q(g, mp)
 
         def lay_q_op(g, mp, copy):
             lay_q(g, mp, qbanks[g, mp], copy)
@@ -419,106 +433,101 @@ def tile_gru_candidate_projection_f7_kernel(
             y_store(m, v, n, ys[m])
 
         units = [(j, 0, MT) for j in range(NF)] + [(j, m0, 2) for m0 in (0, 2) for j in range(NF, JT)]
-        pend_turn = []
-
-        def q_ops(g, mp):
-            js = range(4 * g, 4 * g + 4)
-            needs = [("q", (j, 0, MT) if j < NF else (j, 2 * mp, 2)) for j in js]
-            op("pe", 4 * 128, turn_q_op, (g, mp), needs, opens=1, name=("turn_q", g, mp))
-            op("act", 540, lay_q_op, (g, mp, SC), [("turn_q", g, mp)], closes=1, name=("lay_q", g, mp))
-            op("dve", 290, quant_q, (g, mp), [("lay_q", g, mp)], name=("qq", g, mp))
-
-        def tail_ops(key):
-            j, m0, nm = key
-            n = nm * P
-            for fn, nm_, need, on_v in ((state_gate, "e", [("d", key), ("z", key)], m0 == 2 and j >= 5), (state_new, "new", [("e", key)], m0 == 2 and j >= 5)):
-                eng, name, cost = (VE, "dve", n + 40) if on_v else (G, "pool", 2.4 * n + 40)
-                op(name, cost, do, (fn, key, eng), need, name=(nm_, key))
+        RUNS = {
+            4: (((4, 0, MT), (5, 0, MT)), ((0, 0, MT), (1, 0, MT))),
+            6: (((6, 0, 2), (7, 0, 2)), ((2, 0, MT), (3, 0, MT))),
+            8: (((6, 2, 2), (7, 2, 2)), ((4, 0, MT),)),
+            9: ((), ((5, 0, MT), (6, 0, 2))),
+        }
+        in_run = [key for run in RUNS.values() for key in run[1]]
 
         def after_turn(key):
             j, m0, nm = key
             n = nm * P
             op("act", n + 40, do, (save_new, key, SC), [("turn_new", key)], name=("save", key))
-            op("dve", n + 40, do, (scale_new, key), [("turn_new", key), ("save", key)], closes=1, name=("q", key))
-            if nm == MT and j % 2 == 1:
-                op("sp", 90, store_new, ((j - 1) * P, 0, MT), [("save", key), ("save", (j - 1, 0, MT))], name=("st", key))
-            if nm == 2 and j % 2 == 1:
+            op("dve", n + 110, do, (scale_new, key), [("turn_new", key), ("save", key)], closes=1, name=("q", key))
+            if j % 2 == 1:
                 other = (j - 1, 0, MT) if j - 1 < NF else (j - 1, m0, 2)
-                op("sp", 90, store_new, ((j - 1) * P, m0, 2), [("save", key), ("save", other)], name=("st", key))
-            if key == (3, 0, MT):
-                q_ops(0, 0)
-                q_ops(0, 1)
-            if j == 3 and nm == 2:
-                q_ops(0, m0 // 2)
-            if j == JT - 1:
-                q_ops(1, m0 // 2)
+                op("sp", 90, store_new, ((j - 1) * P, m0, nm), [("save", key), ("save", other)], name=("st", key))
+
+        def q_ops(g, mps, needs):
+            op("pe", 4 * 100 * len(mps), turns_op, ((), (), [(g, mp) for mp in mps]), needs, opens=len(mps), name=("turn_q", g, mps))
+            for mp in mps:
+                op("act", 540, lay_q_op, (g, mp, SC), [("turn_q", g, mps)], closes=1, name=("lay_q", g, mp))
+                op("dve", 290, quant_q, (g, mp), [("lay_q", g, mp)], name=("qq", g, mp))
 
         def y_ops(m):
             mp = m // 2
             for v in range(4):
-                op("pe", 262, y_op, (m, v, 0), [("qq", 0, mp)], opens=1, name=("y0", m, v))
+                op("pe", 262, y_op, (m, v, 0), [("qq", 0, mp)], opens=1, name=("y0", m, v), keep=3)
             for v in range(4):
                 op("pe", 262, y_op, (m, v, 1), [("qq", 1, mp), ("y0", m, v)], name=("y1", m, v))
-                if v == 1:
+                if False:
                     op("act", 545, y_copy_op, (m, v), [("y1", m, v)], closes=1, name=("yc", m, v))
                     op("pool", 1270, y_bias_op, (m, v), [("yc", m, v)], name=("ya", m, v))
                 else:
                     op("dve", 555, y_add_op, (m, v), [("y1", m, v)], closes=1, name=("ya", m, v))
-            for v in range(0, 4, 1):
-                op("sp", 90, y_store_op, (m, v, 1), [("ya", m, x) for x in range(v, v + 1)], name=("ys", m, v))
+            w = 1
+            for v in range(0, 4, w):
+                op("sp", 90, y_store_op, (m, v, w), [("ya", m, x) for x in range(v, v + w)], name=("ys", m, v))
 
-        def run_op(key, others):
-            turn_h_state(*key)
-            for other in others:
-                turn_new(live[other])
-
-        with_run = {}
-        for at, key in enumerate(units):
-            k = at + (3 if key[2] == MT else 5)
-            with_run.setdefault(units[k] if k < len(units) else None, []).append(key)
         for at, key in enumerate(units):
             j, m0, nm = key
             n = nm * P
             half = nm == 2
-            k = 78 * 2 if half else 262
+            k = 84 * 2 if half else 272
             room = [("d", units[at - 3])] if at >= 3 else []
-            if j > 0:
-                if half:
-                    op("pe", 5 * k, mm_op, (key, ("r", "ch")), room, opens=1, name=("rch", key))
-                    op("pe", 4 * k, mm_op, (key, ("cx", "z")), [], opens=1, name=("cxz", key))
-                    where["r", key] = where["ch", key] = where["rch", key]
-                    where["cx", key] = where["zz", key] = where["cxz", key]
-                else:
-                    op("pe", 3 * k, mm_op, (key, ("r",)), room, opens=1, name=("r", key))
-                    op("pe", 2 * k, mm_op, (key, ("ch",)), [], opens=1, name=("ch", key))
-                    op("pe", k, mm_op, (key, ("cx",)), [], opens=1, name=("cx", key))
-                    op("pe", 3 * k, mm_op, (key, ("z",)), [], opens=1, name=("zz", key))
-                others = tuple(with_run.get(key, []))
-                op("pe", 64 * nm + sum(104 * x[2] for x in others), run_op, (key, others), [("new", x) for x in others], opens=1 + len(others), name=("hT", key))
-                for x in others:
-                    where["turn_new", x] = where["hT", key]
-                    after_turn(x)
-            else:
-                op("pe", 1, len, ((),), [], opens=5, name=("r", key))
+            if at == 0:
+                op("pe", 1, len, ((),), [], opens=6, name=("r", key))
                 for x in ("ch", "cx", "zz", "hT"):
                     where[x, key] = where["r", key]
+                for jj in (1, 2, 3):
+                    where["hT", (jj, 0, MT)] = where["r", key]
+            elif half:
+                op("pe", 5 * k, mm_op, (key, ("r", "ch")), room, opens=1, name=("r", key))
+                where["ch", key] = where["r", key]
+            else:
+                op("pe", 3 * k, mm_op, (key, ("r",)), room, opens=1, name=("r", key))
+                op("pe", 2 * k, mm_op, (key, ("ch",)), [], opens=1, name=("ch", key))
+                op("pe", k, mm_op, (key, ("cx",)), [], opens=1, name=("cx", key))
+            if at in RUNS:
+                states, news = RUNS[at]
+                opens = (1 if states else 0) + len(news)
+                cost = sum([64 * x[2] for x in states] + [85 * x[2] for x in news])
+                op("pe", cost, turns_op, (states, news, ()), [("new", x) for x in news], opens=opens, name=("run", at))
+                for x in states:
+                    where["hT", x] = where["run", at]
+                for x in news:
+                    where["turn_new", x] = where["run", at]
+                    after_turn(x)
+            if half:
+                op("pe", 4 * k, mm_op, (key, ("cx", "z")), [], opens=1, name=("cx", key))
+                where["zz", key] = where["cx", key]
+            elif at > 0:
+                op("pe", 3 * k, mm_op, (key, ("z",)), [], opens=1, name=("zz", key))
             op("act", n + 40, sig_op, (key, "r", 0), [("r", key)], closes=0 if half else 1, name=("sr", key))
             op("dve", n + 45, do, (cand_in, key), [("sr", key), ("ch", key)], closes=1, name=("t1", key))
             op("dve", n + 45, do, (cand_sum, key), [("t1", key), ("cx", key)], closes=0 if half else 1, name=("t2", key))
             op("act", n + 40, do, (cand_tanh, key), [("t2", key)], name=("cand", key))
             op("act", n + 40, sig_op, (key, "z", 1), [("zz", key)] + ([("t2", key)] if half else []), closes=1, name=("z", key))
-            op("dve", n + 45, do, (state_diff, key), [("cand", key), ("hT", key)], closes=1, name=("d", key))
-            tail_ops(key)
-        for key in with_run.get(None, []):
-            op("pe", 104 * key[2], do, (turn_new, key), [("new", key)], opens=1, name=("turn_new", key))
-            after_turn(key)
+            op("dve", n + 45, do, (state_diff, key), [("cand", key), ("hT", key)], closes=1 if j % 2 else 0, name=("d", key))
+            for fn, what, needs, on_v in ((state_gate, "e", [("d", key), ("z", key)], m0 == 2), (state_new, "new", [("e", key)], m0 == 2)):
+                eng, name, cost = (VE, "dve", n + 40) if on_v else (G, "pool", 2.4 * n + 40)
+                op(name, cost, do, (fn, key, eng), needs, name=(what, key))
+            if at == 9:
+                q_ops(0, (0, 1), [("q", (jj, 0, MT)) for jj in range(4)])
+        for key in units:
+            if key not in in_run:
+                op("pe", 85 * key[2], turns_op, ((), (key,), ()), [("new", key)], opens=1, name=("turn_new", key))
+                after_turn(key)
+                if key[0] == JT - 1:
+                    q_ops(1, (key[1] // 2,), [("q", (jj, 0, MT) if jj < NF else (jj, key[1], 2)) for jj in range(4, 8)])
         for m in range(MT):
             y_ops(m)
 
         free = {}
         end = [None] * len(ops)
-        kinds = [o[0] for o in ops]
-        pending = {e: [i for i in range(len(ops)) if kinds[i] == e] for e in ("pe", "act", "dve", "pool", "sp")}
+        pending = {e: [i for i in range(len(ops)) if ops[i][0] == e] for e in ("pe", "act", "dve", "pool", "sp")}
         used, release = 0, []
         order = []
         while any(pending.values()):
@@ -526,17 +535,16 @@ def tile_gru_candidate_projection_f7_kernel(
             for e, queue in pending.items():
                 t0 = free.get(e, 0)
                 pick = None
-                for i in queue[:60]:
+                for i in queue:
                     o = ops[i]
                     if any(end[x] is None for x in o[4]):
                         continue
-                    t = max([t0] + [end[x] + (0 if kinds[x] == e == "pe" else 460 if kinds[x] == "pe" else 250) for x in o[4]])
+                    t = max([t0] + [end[x] + (0 if ops[x][0] == e == "pe" else 460 if ops[x][0] == "pe" else 250) for x in o[4]])
                     spare = 8 - used
+                    if o[5] and spare + len(release) < o[5] + o[7]:
+                        continue
                     if o[5] > spare:
-                        short = o[5] - spare
-                        if short > len(release):
-                            continue
-                        t = max(t, sorted(release)[short - 1] + 250)
+                        t = max(t, sorted(release)[o[5] - spare - 1] + 250)
                     if pick is None or t < pick[0]:
                         pick = (t, i)
                     if t == t0:
@@ -548,8 +556,7 @@ def tile_gru_candidate_projection_f7_kernel(
             pending[e].remove(i)
             order.append(i)
             if o[5]:
-                spare = 8 - used
-                short = max(0, o[5] - spare)
+                short = max(0, o[5] - (8 - used))
                 release = sorted(release)[short:]
                 used += o[5] - short
             free[e] = t + o[1]

@@ -1,4 +1,5 @@
 from contextlib import ExitStack
+from functools import partial
 
 import concourse.mybir as mybir
 from concourse.masks import make_identity
@@ -8,7 +9,7 @@ BF16 = mybir.dt.bfloat16
 I32 = mybir.dt.int32
 U32 = mybir.dt.uint32
 U8 = mybir.dt.uint8
-FP8 = mybir.dt.float8_e4m3fn
+E4M3 = mybir.dt.float8_e4m3fn
 E4M3X4 = mybir.dt.float8_e4m3fn_x4
 E2M1X4 = mybir.dt.float4_e2m1fn_x4
 ACT = mybir.ActivationFunctionType
@@ -16,10 +17,61 @@ ALU = mybir.AluOpType
 
 B, D, H, V = 512, 512, 1024, 2048
 P = 128
-MT = B // P
-JT = H // P
-G_OF_H = H // 512
+TOKEN_TILES = B // P
+CHANNEL_TILES = H // P
+BANK = 512
+Y_TILES = V // BANK
+BANKS = 8
 FLOPS = 2 * B * (D * 3 * H + H * 3 * H + H * V)
+
+RESET, UPDATE, CANDIDATE = 0, 1, 2
+SUMS = {"reset": (RESET, (0, 1, 2)), "hc": (CANDIDATE, (0, 1)), "xc": (CANDIDATE, (2,)), "update": (UPDATE, (0, 1, 2))}
+EARLY_TILES = 2
+HEAD_TILES = 4
+
+LAST = CHANNEL_TILES - 1
+WHOLE = [(j, 0, TOKEN_TILES) for j in range(LAST)]
+HALVES = [(LAST, 0, 2), (LAST, 2, 2)]
+
+
+def plan_order(steps):
+    tensor_lag, lag = 460, 200
+    engine_free = {"tensor": 0, "scalar": 0, "vector": 0, "gpsimd": 0, "sync": 0}
+    waiting = {engine: [i for i, step in enumerate(steps) if step[0] == engine] for engine in engine_free}
+    end = [None] * len(steps)
+    taken, returned = 0, []
+    order = []
+    while any(waiting.values()):
+        best = None
+        for engine, queue in waiting.items():
+            pick = None
+            for i in queue:
+                after, opens, spare = steps[i][3], steps[i][4], steps[i][6]
+                if any(end[x] is None for x in after):
+                    continue
+                start = engine_free[engine]
+                for x in after:
+                    on_tensor = steps[x][0] == "tensor"
+                    start = max(start, end[x] + (0 if on_tensor and engine == "tensor" else tensor_lag if on_tensor else lag))
+                free = BANKS - taken
+                if opens and free + len(returned) < opens + spare:
+                    continue
+                if opens > free:
+                    start = max(start, sorted(returned)[opens - free - 1] + lag)
+                if pick is None or start < pick[0]:
+                    pick = (start, i)
+            if pick and (best is None or pick[0] < best[0]):
+                best = pick
+        start, i = best
+        engine, cost, call, after, opens, frees, spare = steps[i]
+        waiting[engine].remove(i)
+        order.append(i)
+        reused = max(0, opens - (BANKS - taken))
+        returned = sorted(returned)[reused:]
+        taken += opens - reused
+        end[i] = engine_free[engine] = start + cost
+        returned += [end[i] + lag] * frees
+    return order
 
 
 def tile_gru_candidate_projection_f7_kernel(
@@ -29,538 +81,455 @@ def tile_gru_candidate_projection_f7_kernel(
     with ExitStack() as ctx:
         keep = ctx.enter_context(tc.tile_pool(name="keep", bufs=1))
         work = ctx.enter_context(tc.tile_pool(name="work", bufs=5))
-        ypool = ctx.enter_context(tc.tile_pool(name="ypool", bufs=3))
-        psum = ctx.enter_context(tc.psum_pool(name="psum", bufs=8))
+        y_pool = ctx.enter_context(tc.tile_pool(name="y_pool", bufs=3))
+        psum = ctx.enter_context(tc.psum_pool(name="psum", bufs=BANKS))
         ctx.enter_context(tc.manual_schedule())
 
-        def bank(dtype=F32):
-            cols = 512 if dtype == F32 else 1024
-            bank_tile = psum.tile([P, cols], dtype, name="bank", tag="bank")
-            return bank_tile
+        def new_bank(dtype=F32):
+            bank = psum.tile([P, BANK if dtype == F32 else 2 * BANK], dtype, name="bank", tag="bank")
+            return bank
 
         ident = keep.tile([P, P], F32, name="ident")
         ident_bf = keep.tile([P, P], BF16, name="ident_bf")
-        rows = keep.tile([P, P], BF16, name="rows")
-        cols = keep.tile([P, 48], F32, name="cols")
-        gain_c = keep.tile([P, JT], BF16, name="gain_c")
-        xs4 = keep.tile([P, 4], F32, name="xs4")
-        xb = keep.tile([P, MT, D], U8, name="xb", align_bytes=64)
-        xf = keep.tile([P, MT, D], BF16, name="xf", align_bytes=64)
-        hsb = keep.tile([P, MT, H], BF16, name="hsb", align_bytes=64)
-        wuA = keep.tile([P, 3, 3, 512], U8, name="wuA", align_bytes=256)
-        wuB = keep.tile([P, 3, 3, 1536], U8, name="wuB", align_bytes=256)
-        us = keep.tile([P, 2, 3 * H], U8, name="us", align_bytes=256)
-        ws = keep.tile([P, 3 * H], U8, name="ws", align_bytes=256)
-        ow = keep.tile([P, 2, V * 4], U8, name="ow", align_bytes=256)
-        osc = keep.tile([P, 2, V], U8, name="osc", align_bytes=256)
-        gain_b = keep.tile([P, H], BF16, name="gain_b")
-        bo_b = keep.tile([P, V], BF16, name="bo_b")
-        junk = keep.tile([P, 1], F32, name="junk")
-        warm = keep.tile([P, 512], BF16, name="warm")
+        warm = keep.tile([P, BANK], BF16, name="warm")
+        table = keep.tile([P, 1], F32, name="table")
+        vec_rows = keep.tile([P, P], BF16, name="vec_rows")
+        vec_cols = keep.tile([P, 6 * CHANNEL_TILES], F32, name="vec_cols")
+        gain_cols = keep.tile([P, CHANNEL_TILES], BF16, name="gain_cols")
+        gain_all = keep.tile([P, H], BF16, name="gain_all")
+        bias_o_all = keep.tile([P, V], BF16, name="bias_o_all")
+        x_codes = keep.tile([P, TOKEN_TILES, D], U8, name="x_codes", align_bytes=64)
+        x_wide = keep.tile([P, TOKEN_TILES, D], BF16, name="x_wide", align_bytes=64)
+        x_scale_4 = keep.tile([P, 4], F32, name="x_scale_4")
+        h_rows = keep.tile([P, TOKEN_TILES, H], BF16, name="h_rows", align_bytes=64)
+        words_early = keep.tile([P, 3, 3, EARLY_TILES * P * 2], U8, name="words_early", align_bytes=256)
+        words_late = keep.tile([P, 3, 3, (CHANNEL_TILES - EARLY_TILES) * P * 2], U8, name="words_late", align_bytes=256)
+        u_bytes = keep.tile([P, 2, 3 * H], U8, name="u_bytes", align_bytes=256)
+        w_bytes = keep.tile([P, 3 * H], U8, name="w_bytes", align_bytes=256)
+        o_codes = keep.tile([P, 2, V * 4], U8, name="o_codes", align_bytes=256)
+        o_bytes = keep.tile([P, 2, V], U8, name="o_bytes", align_bytes=256)
+        h_in = keep.tile([P, 2, B, 4], BF16, name="h_in", align_bytes=64)
+        x_in = keep.tile([P, B, 4], BF16, name="x_in", align_bytes=64)
+        q_in = keep.tile([P, 2, B, 4], BF16, name="q_in", align_bytes=64)
+        hx_codes = keep.tile([P, 3, B], U32, name="hx_codes", align_bytes=256)
+        hx_bytes = keep.tile([P, 3, B], U8, name="hx_bytes", align_bytes=256)
+        q_codes = keep.tile([P, 2, B], U32, name="q_codes", align_bytes=256)
+        q_bytes = keep.tile([P, 2, B], U8, name="q_bytes", align_bytes=256)
+        new_rows = keep.tile([P, TOKEN_TILES, H], F32, name="new_rows")
+        q_rows = keep.tile([P, TOKEN_TILES, 2, 2, P, 2], BF16, name="q_rows", align_bytes=64)
 
-        nc.vector.memset(junk[:], 0.0)
+        nc.vector.memset(table[:], 0.0)
         nc.vector.memset(warm[:], 0.0)
-        nc.vector.memset(rows[:], 0.0)
-        nc.vector.memset(us[:].rearrange("p g n -> p (g n)").bitcast(I32), 0)
-        nc.vector.memset(ws[:].bitcast(I32), 0)
-        nc.vector.memset(osc[:].rearrange("p g n -> p (g n)").bitcast(I32), 0)
+        nc.vector.memset(vec_rows[:], 0.0)
+        nc.vector.memset(u_bytes[:].rearrange("p g n -> p (g n)").bitcast(I32), 0)
+        nc.vector.memset(w_bytes[:].bitcast(I32), 0)
+        nc.vector.memset(o_bytes[:].rearrange("p g n -> p (g n)").bitcast(I32), 0)
         make_identity(nc, ident[:])
         nc.gpsimd.tensor_copy(out=ident_bf[:], in_=ident[:])
         first_row = 0
-        for vec in (gain, bias, bias_c, carry):
-            n = vec.shape[0] // P
-            nc.gpsimd.dma_start(out=rows[first_row : first_row + n, :], in_=vec.rearrange("(r c) -> r c", c=P))
-            first_row += n
+        for vector in (gain, bias, bias_c, carry):
+            rows = vector.shape[0] // P
+            nc.gpsimd.dma_start(out=vec_rows[first_row : first_row + rows, :], in_=vector.rearrange("(r c) -> r c", c=P))
+            first_row += rows
 
         h_view = h.rearrange("(m p) d -> p m d", p=P)
-        def load_wu(dst, lo, hi, gs):
-            for g in gs:
-                src = u_words[g] if g < 2 else w_words[0]
-                nc.sync.dma_start(out=dst[:, g, :, :], in_=src.rearrange("p (s n) -> p s n", s=3)[:, :, lo:hi])
 
-        nc.sync.dma_start(out=hsb[:, 0, :], in_=h_view[:, 0, :])
-        nc.sync.dma_start(out=xb[:], in_=x_bytes.rearrange("(m p) d -> p m d", p=P))
-        nc.sync.dma_start(out=hsb[:, 1, :], in_=h_view[:, 1, :])
-        nc.scalar.dma_start(out=xs4[:], in_=x_scale.rearrange("o (p t) -> p (o t)", t=4))
-        nc.scalar.activation(out=junk[:], in_=junk[:], func=ACT.Sigmoid)
-        for r in range(4):
-            nc.sync.dma_start(out=us[r:P:32, :, :].bitcast(I32), in_=u_scales.rearrange("g (b r) n -> r b g n", r=4)[r].bitcast(I32))
-        load_wu(wuA, 0, 512, (0, 1, 2))
-        nc.sync.dma_start(out=hsb[:, 2:4, :], in_=h_view[:, 2:4, :])
-        for r in range(4):
-            nc.sync.dma_start(out=ws[r:P:32, :].bitcast(I32), in_=w_scales.rearrange("g (b r) n -> r b (g n)", r=4)[r].bitcast(I32))
-        load_wu(wuB, 512, 2048, (0, 1, 2))
-        for r in range(4):
-            nc.sync.dma_start(out=osc[r:P:32, :, :].bitcast(I32), in_=o_scales.rearrange("g (b r) n -> r b g n", r=4)[r].bitcast(I32))
+        def load_words(tile, first, last, groups):
+            for g in groups:
+                source = u_words[g] if g < 2 else w_words[0]
+                part_view = source.rearrange("p (part n) -> p part n", part=3)
+                nc.sync.dma_start(out=tile[:, g, :, :], in_=part_view[:, :, first * 2 * P : last * 2 * P])
+
+        def load_scale_rows(tile_rows, scales):
+            view = scales.rearrange("g (b r) n -> r b g n", r=4)
+            for r in range(4):
+                nc.sync.dma_start(out=tile_rows[r:P:32, :, :].bitcast(I32), in_=view[r].bitcast(I32))
+
+        nc.sync.dma_start(out=h_rows[:, 0, :], in_=h_view[:, 0, :])
+        nc.sync.dma_start(out=x_codes[:], in_=x_bytes.rearrange("(m p) d -> p m d", p=P))
+        nc.sync.dma_start(out=h_rows[:, 1, :], in_=h_view[:, 1, :])
+        nc.scalar.dma_start(out=x_scale_4[:], in_=x_scale.rearrange("o (p t) -> p (o t)", t=4))
+        nc.scalar.activation(out=table[:], in_=table[:], func=ACT.Sigmoid)
+        load_scale_rows(u_bytes, u_scales)
+        load_words(words_early, 0, EARLY_TILES, (0, 1, 2))
+        nc.sync.dma_start(out=h_rows[:, 2:4, :], in_=h_view[:, 2:4, :])
+        load_scale_rows(w_bytes[:].rearrange("p (o n) -> p o n", o=1), w_scales)
+        load_words(words_late, EARLY_TILES, CHANNEL_TILES, (0, 1, 2))
+        load_scale_rows(o_bytes, o_scales)
         for g in range(2):
+            o_view = o_words[g].rearrange("p n t -> p (n t)")
             for half in range(2):
-                ps = slice(4096 * half, 4096 * half + 4096)
-                nc.sync.dma_start(out=ow[:, g, ps].bitcast(I32), in_=o_words[g].rearrange("p n t -> p (n t)")[:, ps].bitcast(I32))
-        nc.sync.dma_start(out=bo_b[:], in_=bias_o.partition_broadcast(P))
-
-        hin = keep.tile([P, 2, B, 4], BF16, name="hin", align_bytes=64)
-        xin = keep.tile([P, B, 4], BF16, name="xin", align_bytes=64)
-        hxc = keep.tile([P, 3, B], U32, name="hxc", align_bytes=256)
-        hxs = keep.tile([P, 3, B], U8, name="hxs", align_bytes=256)
-        hin_words = hin[:].rearrange("p g r t -> p g (r t)").bitcast(F32)
-
-        def widen_x(m, copy):
-            copy(out=xf[:, m, :], in_=xb[:, m, :].bitcast(FP8))
-
-        def dummy(n):
-            t = bank()
-            for i in range(n):
-                nc.tensor.matmul(t[:], lhsT=warm[:, 0:P], rhs=warm[:], start=True, stop=True)
+                cols = slice(half * 2 * V, (half + 1) * 2 * V)
+                nc.sync.dma_start(out=o_codes[:, g, cols].bitcast(I32), in_=o_view[:, cols].bitcast(I32))
+        nc.sync.dma_start(out=bias_o_all[:], in_=bias_o.partition_broadcast(P))
 
         def turn_h(m):
-            words = hsb[:, m, :].bitcast(F32)
-            t = bank()
+            bank = new_bank()
+            words = h_rows[:, m, :].bitcast(F32)
             for g in range(2):
                 for u in range(2):
                     i = 2 * g + u
-                    nc.tensor.transpose(t[:, i * P : (i + 1) * P], words[:, 256 * g + u : 256 * (g + 1) : 2], ident[:])
-            return t
+                    nc.tensor.transpose(bank[:, i * P : (i + 1) * P], words[:, 256 * g + u : 256 * (g + 1) : 2], ident[:])
+            return bank
 
-        def turn_x(mp):
-            t = bank()
-            for mm in range(2):
-                words = xf[:, 2 * mp + mm, :].bitcast(F32)
+        def lay_h(m, bank, copy):
+            words = h_in[:].rearrange("p g r t -> p g (r t)").bitcast(F32)
+            to = words[:, :, m * 2 * P : (m + 1) * 2 * P].rearrange("p g (r u) -> p g r u", u=2)
+            copy(out=to, in_=bank[:].rearrange("p (g u r) -> p g r u", g=2, u=2))
+
+        def quantize_h(m):
+            tokens = slice(m * P, (m + 1) * P)
+            for g in range(2):
+                nc.vector.quantize_mx(
+                    out=hx_codes[:, g, tokens].bitcast(E4M3X4),
+                    scales=hx_bytes[:, g, tokens],
+                    in_=h_in[:, g, tokens, :].rearrange("p r t -> p (r t)"),
+                )
+
+        def turn_x(pair):
+            bank = new_bank()
+            for m in range(2):
+                words = x_wide[:, 2 * pair + m, :].bitcast(F32)
                 for u in range(2):
-                    i = 2 * mm + u
-                    nc.tensor.transpose(t[:, i * P : (i + 1) * P], words[:, u:256:2], ident[:])
-            return t
+                    i = 2 * m + u
+                    nc.tensor.transpose(bank[:, i * P : (i + 1) * P], words[:, u : 2 * P : 2], ident[:])
+            return bank
 
-        def lay_h(m, t, copy):
-            dst = hin_words[:, :, m * 256 : (m + 1) * 256].rearrange("p g (r u) -> p g r u", u=2)
-            copy(out=dst, in_=t[:].rearrange("p (g u r) -> p g r u", g=2, u=2))
-
-        def lay_x(mp, t):
-            scales = xs4[:].rearrange("p (u e) -> p u e", e=2).unsqueeze(1).to_broadcast([P, P, 2, 2])
-            for mm in range(2):
-                m = 2 * mp + mm
+        def scale_x(pair, bank):
+            scales = x_scale_4[:].rearrange("p (u e) -> p u e", e=2).unsqueeze(1).to_broadcast([P, P, 2, 2])
+            for m in range(2):
+                first = (2 * pair + m) * P
                 nc.vector.tensor_tensor(
-                    out=xin[:, m * P : (m + 1) * P, :].rearrange("p r (u e) -> p r u e", e=2),
-                    in0=t[:, 256 * mm : 256 * (mm + 1)].bitcast(BF16).rearrange("p (u r e) -> p r u e", u=2, e=2),
+                    out=x_in[:, first : first + P, :].rearrange("p r (u e) -> p r u e", e=2),
+                    in0=bank[:, 2 * P * m : 2 * P * (m + 1)].bitcast(BF16).rearrange("p (u r e) -> p r u e", u=2, e=2),
                     in1=scales,
                     op=ALU.mult,
                 )
 
-        def quant_h(m):
-            rs = slice(m * P, (m + 1) * P)
-            for g in range(2):
-                nc.vector.quantize_mx(
-                    out=hxc[:, g, rs].bitcast(E4M3X4), scales=hxs[:, g, rs], in_=hin[:, g, rs, :].rearrange("p r t -> p (r t)")
-                )
+        def quantize_x(pair):
+            tokens = slice(pair * 2 * P, (pair + 1) * 2 * P)
+            nc.vector.quantize_mx(
+                out=hx_codes[:, 2, tokens].bitcast(E4M3X4),
+                scales=hx_bytes[:, 2, tokens],
+                in_=x_in[:, tokens, :].rearrange("p r t -> p (r t)"),
+            )
 
-        def quant_x(mp):
-            rs = slice(mp * 256, (mp + 1) * 256)
-            nc.vector.quantize_mx(out=hxc[:, 2, rs].bitcast(E4M3X4), scales=hxs[:, 2, rs], in_=xin[:, rs, :].rearrange("p r t -> p (r t)"))
+        def column(vector, j):
+            i = (vector + 1) * CHANNEL_TILES + j
+            return vec_cols[:, i : i + 1]
 
-        bias_col = lambda part, j: cols[:, (part + 1) * JT + j : (part + 1) * JT + j + 1]
-        PART_BC, PART_CARRY = 3, 4
+        BIAS_C, CARRY = 3, 4
 
-        def wu_slice(g, s, j):
-            c = j * 256
-            src = wuA[:, g, s, c : c + 256] if j < 2 else wuB[:, g, s, c - 512 : c - 256]
-            return src.bitcast(E2M1X4)
-
-        def gate_mm(out, s, j, groups, rs):
-            c = s * H + j * P
-            for i, g in enumerate(groups):
+        def sum_passes(out, name, j, tokens):
+            part, groups = SUMS[name]
+            c = part * H + j * P
+            for g in groups:
+                tile, first = (words_early, j) if j < EARLY_TILES else (words_late, j - EARLY_TILES)
                 nc.tensor.matmul_mx(
                     out=out,
-                    lhsT=wu_slice(g, s, j),
-                    lhsT_scale=us[:, g, c : c + P] if g < 2 else ws[:, c : c + P],
-                    rhs=hxc[:, g, rs].bitcast(E4M3X4),
-                    rhs_scale=hxs[:, g, rs],
-                    start=(i == 0),
-                    stop=(i == len(groups) - 1),
+                    lhsT=tile[:, g, part, first * 2 * P : (first + 1) * 2 * P].bitcast(E2M1X4),
+                    lhsT_scale=u_bytes[:, g, c : c + P] if g < 2 else w_bytes[:, c : c + P],
+                    rhs=hx_codes[:, g, tokens].bitcast(E4M3X4),
+                    rhs_scale=hx_bytes[:, g, tokens],
+                    start=(g == groups[0]),
+                    stop=(g == groups[-1]),
                 )
 
-        newo = keep.tile([P, MT, H], F32, name="newo")
-        qb = keep.tile([P, MT, 2, 2, P, 2], BF16, name="qb", align_bytes=64)
-        qin = keep.tile([P, 2, B, 4], BF16, name="qin", align_bytes=64)
-        qc = keep.tile([P, 2, B], U32, name="qc", align_bytes=256)
-        qs = keep.tile([P, 2, B], U8, name="qs", align_bytes=256)
-        qin_words = qin[:].rearrange("p g r t -> p g (r t)").bitcast(F32)
-        new_out = out_1.rearrange("(m p) c -> p m c", p=P)
-        y_out = out_0.rearrange("(m p) v -> p m v", p=P)
+        sums = {}
+        states = {}
+        slabs = {}
 
-        GATES = {"r": (0, (0, 1, 2)), "ch": (2, (0, 1)), "cx": (2, (2,)), "z": (1, (0, 1, 2))}
+        def sum_all(name, j):
+            sums[name, j] = new_bank()
+            sum_passes(sums[name, j][:], name, j, slice(0, B))
 
-        class_free = None
+        def of(slab, name):
+            tiles = slabs.setdefault(slab, {})
+            if name not in tiles:
+                tiles[name] = work.tile([P, B], F32, name=name, tag=name)
+            return tiles[name][:, 0 : slab[2] * P]
 
-        def start_unit(j, m0, nm):
-            u = {"j": j, "m0": m0, "nm": nm, "n": nm * P, "cs": slice(m0 * P, (m0 + nm) * P)}
-            for name in ("r", "z", "t1", "t2", "cand", "d", "e", "new"):
-                made = work.tile([P, B], F32, name=name, tag=name)
-                u[name] = made[:, 0 : u["n"]]
-            return u
+        def sum_of(slab, name):
+            return sums[name, slab[0]][:, slab[1] * P : (slab[1] + slab[2]) * P]
 
-        def mm_full(u, names):
-            for name in names:
-                s, groups = GATES[name]
-                t = bank()
-                gate_mm(t[:], s, u["j"], groups, slice(0, B))
-                u["p_" + name] = t[:]
+        def gate(slab, name, part):
+            nc.scalar.activation(out=of(slab, name), in_=sum_of(slab, name), func=ACT.Sigmoid, bias=column(part, slab[0]))
 
-        def mm_tiles(u, names_of_bank, ms):
-            n = u["n"]
-            for names in names_of_bank:
-                if "p_" + names[0] not in u:
-                    t = bank()
-                    for i, name in enumerate(names):
-                        u["p_" + name] = t[:, i * n : (i + 1) * n]
-            for m in ms:
-                k = m - u["m0"]
-                for names in names_of_bank:
-                    for name in names:
-                        s, groups = GATES[name]
-                        gate_mm(u["p_" + name][:, k * P : (k + 1) * P], s, u["j"], groups, slice(m * P, (m + 1) * P))
-
-        def sig(u, name, s):
-            nc.scalar.activation(out=u[name], in_=u["p_" + name], func=ACT.Sigmoid, bias=bias_col(s, u["j"]))
-
-        def cand_in(u):
+        def reset_hc(slab):
             nc.vector.scalar_tensor_tensor(
-                out=u["t1"], in0=u["p_ch"], scalar=bias_col(PART_BC, u["j"]), in1=u["r"], op0=ALU.add, op1=ALU.mult
+                out=of(slab, "rh"), in0=sum_of(slab, "hc"), scalar=column(BIAS_C, slab[0]), in1=of(slab, "reset"), op0=ALU.add, op1=ALU.mult
             )
 
-        def cand_sum(u):
-            nc.vector.tensor_tensor(out=u["t2"], in0=u["p_cx"], in1=u["t1"], op=ALU.add)
+        def add_xc(slab):
+            nc.vector.tensor_tensor(out=of(slab, "pre"), in0=sum_of(slab, "xc"), in1=of(slab, "rh"), op=ALU.add)
 
-        def cand_tanh(u):
-            nc.scalar.activation(out=u["cand"], in_=u["t2"], func=ACT.Tanh, bias=bias_col(2, u["j"]))
+        def candidate(slab):
+            nc.scalar.activation(out=of(slab, "cand"), in_=of(slab, "pre"), func=ACT.Tanh, bias=column(CANDIDATE, slab[0]))
 
-        HT = {}
-
-        def turn_states(keys):
-            t = bank(BF16)
-            c = 0
-            for j, m0, nm in keys:
-                HT[j, m0] = t[:, c : c + nm * P]
-                for m in range(m0, m0 + nm):
-                    nc.tensor.transpose(t[:, c : c + P], hsb[:, m, j * P : (j + 1) * P], ident_bf[:])
-                    c += P
-
-        def state_diff(u):
+        def difference(slab):
             nc.vector.scalar_tensor_tensor(
-                out=u["d"], in0=HT[u["j"], u["m0"]], scalar=bias_col(PART_CARRY, u["j"]), in1=u["cand"], op0=ALU.mult, op1=ALU.subtract
+                out=of(slab, "diff"), in0=states[slab], scalar=column(CARRY, slab[0]), in1=of(slab, "cand"), op0=ALU.mult, op1=ALU.subtract
             )
 
-        def state_gate(u, eng):
-            eng.tensor_tensor(out=u["e"], in0=u["z"], in1=u["d"], op=ALU.mult)
+        def times_update(engine, slab):
+            engine.tensor_tensor(out=of(slab, "step"), in0=of(slab, "update"), in1=of(slab, "diff"), op=ALU.mult)
 
-        def state_new(u, eng):
-            eng.tensor_tensor(out=u["new"], in0=u["cand"], in1=u["e"], op=ALU.add)
+        def new_state(engine, slab):
+            engine.tensor_tensor(out=of(slab, "new"), in0=of(slab, "cand"), in1=of(slab, "step"), op=ALU.add)
 
-        def turn_new(u):
-            t = bank()
-            for k in range(u["nm"]):
-                nc.tensor.transpose(t[:, k * P : (k + 1) * P], u["new"][:, k * P : (k + 1) * P], ident[:])
-            u["newT"] = t[:, 0 : u["n"]].rearrange("p (m c) -> p m c", c=P)
+        def turn_state(out, j, m):
+            nc.tensor.transpose(out, h_rows[:, m, j * P : (j + 1) * P], ident_bf[:])
 
-        def scale_new(u):
-            g, p0 = u["j"] // 4, u["j"] % 4 * 32
-            ms = slice(u["m0"], u["m0"] + u["nm"])
-            by_word = u["newT"].rearrange("p m (k w e) -> p m w k e", w=2, e=2)
-            gain_v = gain_b[:, u["j"] * P : (u["j"] + 1) * P].rearrange("p (k w e) -> p w k e", w=2, e=2)
-            for w in range(2):
+        turned = {}
+        q_banks = {}
+        new_view = out_1.rearrange("(m p) c -> p m c", p=P)
+        y_view = out_0.rearrange("(m p) v -> p m v", p=P)
+
+        def turn_run(states_of, news_of, q_of):
+            if states_of:
+                bank = new_bank(BF16)
+                at = 0
+                for slab in states_of:
+                    states[slab] = bank[:, at : at + slab[2] * P]
+                    for m in range(slab[1], slab[1] + slab[2]):
+                        turn_state(bank[:, at : at + P], slab[0], m)
+                        at += P
+            for slab in news_of:
+                bank = new_bank()
+                for m in range(slab[2]):
+                    nc.tensor.transpose(bank[:, m * P : (m + 1) * P], of(slab, "new")[:, m * P : (m + 1) * P], ident[:])
+                turned[slab] = bank[:, 0 : slab[2] * P].rearrange("p (m c) -> p m c", c=P)
+            for g, pair in q_of:
+                bank = new_bank()
+                for m in range(2):
+                    for u in range(2):
+                        i = 2 * m + u
+                        words = q_rows[:, 2 * pair + m, g, u, :, :].rearrange("p k e -> p (k e)").bitcast(F32)
+                        nc.tensor.transpose(bank[:, i * P : (i + 1) * P], words, ident[:])
+                q_banks[g, pair] = bank
+
+        def keep_new(slab):
+            j, m, n = slab
+            nc.scalar.copy(out=new_rows[:, m : m + n, j * P : (j + 1) * P], in_=turned[slab])
+
+        def times_gain(slab):
+            j, m, n = slab
+            g, first = j // 4, j % 4 * (P // 4)
+            by_u = turned[slab].rearrange("p m (k u e) -> p m u k e", u=2, e=2)
+            gain_by_u = gain_all[:, j * P : (j + 1) * P].rearrange("p (k u e) -> p u k e", u=2, e=2)
+            for u in range(2):
                 nc.vector.tensor_tensor(
-                    out=qb[:, ms, g, w, p0 : p0 + 32, :],
-                    in0=by_word[:, :, w, :, :],
-                    in1=gain_v[:, w, :, :].unsqueeze(1).to_broadcast([P, u["nm"], 32, 2]),
+                    out=q_rows[:, m : m + n, g, u, first : first + P // 4, :],
+                    in0=by_u[:, :, u, :, :],
+                    in1=gain_by_u[:, u, :, :].unsqueeze(1).to_broadcast([P, n, P // 4, 2]),
                     op=ALU.mult,
                 )
 
-        def save_new(u, copy):
-            cs = slice(u["j"] * P, (u["j"] + 1) * P)
-            copy(out=newo[:, u["m0"] : u["m0"] + u["nm"], cs], in_=u["newT"])
+        def lay_q(g, pair):
+            words = q_in[:].rearrange("p g r t -> p g (r t)").bitcast(F32)
+            to = words[:, g, pair * 4 * P : (pair + 1) * 4 * P].rearrange("p (m r u) -> p m r u", m=2, u=2)
+            nc.scalar.copy(out=to, in_=q_banks[g, pair][:].rearrange("p (m u r) -> p m r u", m=2, u=2))
 
-        def turn_q(g, mp):
-            t = bank()
-            for mm in range(2):
-                for u in range(2):
-                    i = 2 * mm + u
-                    words = qb[:, 2 * mp + mm, g, u, :, :].rearrange("p k e -> p (k e)").bitcast(F32)
-                    nc.tensor.transpose(t[:, i * P : (i + 1) * P], words, ident[:])
-            return t
-
-        def lay_q(g, mp, t, copy):
-            dst = qin_words[:, g, mp * 512 : (mp + 1) * 512].rearrange("p (m r u) -> p m r u", m=2, u=2)
-            copy(out=dst, in_=t[:].rearrange("p (m u r) -> p m r u", m=2, u=2))
-
-        def quant_q(g, mp):
-            rs = slice(mp * 256, (mp + 1) * 256)
-            nc.vector.quantize_mx(out=qc[:, g, rs].bitcast(E4M3X4), scales=qs[:, g, rs], in_=qin[:, g, rs, :].rearrange("p r t -> p (r t)"))
-
-        def store_new(c0, m0, nm):
-            nc.sync.dma_start(out=new_out[:, m0 : m0 + nm, c0 : c0 + 256], in_=newo[:, m0 : m0 + nm, c0 : c0 + 256])
-
-        def y_mm(m, v, groups, t):
-            for g in groups:
-                nc.tensor.matmul_mx(
-                    out=t[:],
-                    lhsT=qc[:, g, m * P : (m + 1) * P].bitcast(E4M3X4),
-                    lhsT_scale=qs[:, g, m * P : (m + 1) * P],
-                    rhs=ow[:, g, v * 2048 : (v + 1) * 2048].bitcast(E4M3X4),
-                    rhs_scale=osc[:, g, v * 512 : (v + 1) * 512],
-                    start=(g == 0),
-                    stop=(g == 1),
-                )
-
-        def y_add(m, v, t, ys):
-            vs = slice(v * 512, (v + 1) * 512)
-            nc.vector.tensor_tensor(out=ys[:, vs], in0=t[:], in1=bo_b[:, vs], op=ALU.add)
-
-        def y_store(m, v, n, ys):
-            ps = slice(v * 512, (v + n) * 512)
-            nc.sync.dma_start(out=y_out[:, m, ps], in_=ys[:, ps])
-
-        G, VE, SC, VC = nc.gpsimd, nc.vector, nc.scalar.copy, nc.vector.tensor_copy
-        state_bank = [bank(BF16), bank(BF16)]
-
-        def head_states(ms):
-            for j in range(4):
-                t = state_bank[j // 2][:, j % 2 * B : (j % 2 + 1) * B]
-                HT[j, 0] = t
-                for m in ms:
-                    nc.tensor.transpose(t[:, m * P : (m + 1) * P], hsb[:, m, j * P : (j + 1) * P], ident_bf[:])
-
-        dummy(4)
-        t_h0 = turn_h(0)
-        lay_h(0, t_h0, SC)
-        widen_x(0, VC)
-        widen_x(1, VC)
-        widen_x(2, VC)
-        widen_x(3, VC)
-        dummy(1)
-        t_x0 = turn_x(0)
-        t_x1 = turn_x(1)
-        t_h1 = turn_h(1)
-        quant_h(0)
-        lay_x(0, t_x0)
-        lay_h(1, t_h1, SC)
-        quant_x(0)
-        quant_h(1)
-        lay_x(1, t_x1)
-        u0 = start_unit(0, 0, 4)
-        FIRST = [("ch",), ("r",), ("cx",), ("z",)]
-        head_states((0, 1))
-        mm_tiles(u0, FIRST, (0, 1))
-        t_h2 = turn_h(2)
-        t_h3 = turn_h(3)
-        lay_h(2, t_h2, SC)
-        quant_x(1)
-        lay_h(3, t_h3, VC)
-        rows_t = bank(BF16)
-        nc.tensor.transpose(rows_t[:, 0:P], rows[:], ident_bf[:])
-        nc.scalar.copy(out=gain_c[:], in_=rows_t[:, 0:JT])
-        nc.scalar.copy(out=cols[:], in_=rows_t[:, 0:48])
-        gain_t = [bank(), bank()]
-        for j in range(JT):
-            nc.tensor.matmul(
-                gain_t[j // 4][:, j % 4 * P : (j % 4 + 1) * P], lhsT=gain_c[:, j : j + 1].to_broadcast([P, P]), rhs=ident_bf[:], start=True, stop=True
+        def quantize_q(g, pair):
+            tokens = slice(pair * 2 * P, (pair + 1) * 2 * P)
+            nc.vector.quantize_mx(
+                out=q_codes[:, g, tokens].bitcast(E4M3X4),
+                scales=q_bytes[:, g, tokens],
+                in_=q_in[:, g, tokens, :].rearrange("p r t -> p (r t)"),
             )
-        quant_h(2)
-        quant_h(3)
-        head_states((2, 3))
-        mm_tiles(u0, FIRST, (2, 3))
-        for c in range(2):
-            nc.scalar.copy(out=gain_b[:, c * 512 : (c + 1) * 512], in_=gain_t[c][:])
 
-        NF = 6
-        ops = []
-        where = {}
+        def store_new(slab):
+            j, m, n = slab
+            cols = slice((j - 1) * P, (j + 1) * P)
+            nc.scalar.dma_start(out=new_view[:, m : m + n, cols], in_=new_rows[:, m : m + n, cols])
 
-        def op(eng, cost, fn, args, needs, opens=0, closes=0, name=None, keep=0):
-            where[name] = len(ops)
-            ops.append((eng, cost, fn, args, [where[x] for x in needs], opens, closes, keep))
+        y_banks = {}
+        y_rows = {}
 
-        live = {(0, 0, MT): u0}
-        ys = {}
-        banks = {}
-        qbanks = {}
-
-        def mm_op(key, names):
-            if key not in live:
-                live[key] = start_unit(*key)
-            u = live[key]
-            if key[2] == MT:
-                mm_full(u, names)
-            else:
-                mm_tiles(u, [names], (key[1], key[1] + 1))
-
-        def sig_op(key, name, s):
-            sig(live[key], name, s)
-
-        def do(fn, key, *args):
-            fn(live[key], *args)
-
-        def turns_op(states, news, qs_):
-            if states:
-                turn_states(states)
-            for key in news:
-                turn_new(live[key])
-            for g, mp in qs_:
-                qbanks[g, mp] = turn_q(g, mp)
-
-        def lay_q_op(g, mp, copy):
-            lay_q(g, mp, qbanks[g, mp], copy)
-
-        def y_op(m, v, g):
+        def y_pass(m, v, g):
             if g == 0:
-                banks[m, v] = bank()
-            y_mm(m, v, (g,), banks[m, v])
+                y_banks[m, v] = new_bank()
+            tokens = slice(m * P, (m + 1) * P)
+            nc.tensor.matmul_mx(
+                out=y_banks[m, v][:],
+                lhsT=q_codes[:, g, tokens].bitcast(E4M3X4),
+                lhsT_scale=q_bytes[:, g, tokens],
+                rhs=o_codes[:, g, v * 4 * BANK : (v + 1) * 4 * BANK].bitcast(E4M3X4),
+                rhs_scale=o_bytes[:, g, v * BANK : (v + 1) * BANK],
+                start=(g == 0),
+                stop=(g == 1),
+            )
 
-        def y_tile(m):
-            if m not in ys:
-                yt = ypool.tile([P, V], F32, name="ys")
-                ys[m] = yt
-            return ys[m]
+        def y_bias(m, v):
+            if m not in y_rows:
+                y_row = y_pool.tile([P, V], F32, name="y_row")
+                y_rows[m] = y_row
+            cols = slice(v * BANK, (v + 1) * BANK)
+            nc.vector.tensor_tensor(out=y_rows[m][:, cols], in0=y_banks[m, v][:], in1=bias_o_all[:, cols], op=ALU.add)
 
-        def y_add_op(m, v):
-            y_add(m, v, banks[m, v], y_tile(m))
+        def y_store(m, v):
+            cols = slice(v * BANK, (v + 1) * BANK)
+            nc.sync.dma_start(out=y_view[:, m, cols], in_=y_rows[m][:, cols])
 
-        def y_copy_op(m, v):
-            nc.scalar.copy(out=y_tile(m)[:, v * 512 : (v + 1) * 512], in_=banks[m, v][:])
+        head_banks = [new_bank(BF16), new_bank(BF16)]
 
-        def y_bias_op(m, v):
-            vs = slice(v * 512, (v + 1) * 512)
-            nc.gpsimd.tensor_tensor(out=ys[m][:, vs], in0=ys[m][:, vs], in1=bo_b[:, vs], op=ALU.add)
+        def turn_head_states(ms):
+            for j in range(HEAD_TILES):
+                state = head_banks[j // 2][:, j % 2 * B : (j % 2 + 1) * B]
+                states[j, 0, TOKEN_TILES] = state
+                for m in ms:
+                    turn_state(state[:, m * P : (m + 1) * P], j, m)
 
-        def y_store_op(m, v, n):
-            y_store(m, v, n, ys[m])
+        def first_sums(ms):
+            for m in ms:
+                for name in ("hc", "reset", "xc", "update"):
+                    if (name, 0) not in sums:
+                        sums[name, 0] = new_bank()
+                    tokens = slice(m * P, (m + 1) * P)
+                    sum_passes(sums[name, 0][:, tokens], name, 0, tokens)
 
-        units = [(j, 0, MT) for j in range(NF)] + [(j, m0, 2) for m0 in (0, 2) for j in range(NF, JT)]
-        RUNS = {
-            4: (((4, 0, MT), (5, 0, MT)), ((0, 0, MT), (1, 0, MT))),
-            6: (((6, 0, 2), (7, 0, 2)), ((2, 0, MT), (3, 0, MT))),
-            8: (((6, 2, 2), (7, 2, 2)), ((4, 0, MT),)),
-            9: ((), ((5, 0, MT), (6, 0, 2))),
-        }
-        in_run = [key for run in RUNS.values() for key in run[1]]
+        def warm_up(passes):
+            bank = new_bank()
+            for i in range(passes):
+                nc.tensor.matmul(bank[:], lhsT=warm[:, 0:P], rhs=warm[:], start=True, stop=True)
 
-        def after_turn(key):
-            j, m0, nm = key
-            n = nm * P
-            op("act", n + 40, do, (save_new, key, SC), [("turn_new", key)], name=("save", key))
-            op("dve", n + 110, do, (scale_new, key), [("turn_new", key), ("save", key)], closes=1, name=("q", key))
-            if j % 2 == 1:
-                other = (j - 1, 0, MT) if j - 1 < NF else (j - 1, m0, 2)
-                op("sp", 90, store_new, ((j - 1) * P, m0, nm), [("save", key), ("save", other)], name=("st", key))
+        scalar_copy, vector_copy = nc.scalar.copy, nc.vector.tensor_copy
+        warm_up(4)
+        h_bank = turn_h(0)
+        lay_h(0, h_bank, scalar_copy)
+        for m in range(TOKEN_TILES):
+            nc.vector.tensor_copy(out=x_wide[:, m, :], in_=x_codes[:, m, :].bitcast(E4M3))
+        warm_up(1)
+        x_banks = [turn_x(0), turn_x(1)]
+        h_bank = turn_h(1)
+        quantize_h(0)
+        scale_x(0, x_banks[0])
+        lay_h(1, h_bank, scalar_copy)
+        quantize_x(0)
+        quantize_h(1)
+        scale_x(1, x_banks[1])
+        turn_head_states((0, 1))
+        first_sums((0, 1))
+        vec_bank = new_bank(BF16)
+        nc.tensor.transpose(vec_bank[:, 0:P], vec_rows[:], ident_bf[:])
+        nc.scalar.copy(out=gain_cols[:], in_=vec_bank[:, 0:CHANNEL_TILES])
+        nc.scalar.copy(out=vec_cols[:], in_=vec_bank[:, 0 : 6 * CHANNEL_TILES])
+        h_banks = [turn_h(2), turn_h(3)]
+        lay_h(2, h_banks[0], scalar_copy)
+        quantize_x(1)
+        lay_h(3, h_banks[1], vector_copy)
+        quantize_h(2)
+        quantize_h(3)
+        turn_head_states((2, 3))
+        gain_banks = [new_bank(), new_bank()]
+        for j in range(CHANNEL_TILES):
+            nc.tensor.matmul(
+                gain_banks[j // 4][:, j % 4 * P : (j % 4 + 1) * P],
+                lhsT=gain_cols[:, j : j + 1].to_broadcast([P, P]),
+                rhs=ident_bf[:],
+                start=True,
+                stop=True,
+            )
+        first_sums((2, 3))
+        for i in range(2):
+            nc.scalar.copy(out=gain_all[:, i * BANK : (i + 1) * BANK], in_=gain_banks[i][:])
 
-        def q_ops(g, mps, needs):
-            op("pe", 4 * 100 * len(mps), turns_op, ((), (), [(g, mp) for mp in mps]), needs, opens=len(mps), name=("turn_q", g, mps))
-            for mp in mps:
-                op("act", 540, lay_q_op, (g, mp, SC), [("turn_q", g, mps)], closes=1, name=("lay_q", g, mp))
-                op("dve", 290, quant_q, (g, mp), [("lay_q", g, mp)], name=("qq", g, mp))
+        steps = []
+        number = {}
 
-        def y_ops(m):
-            mp = m // 2
-            for v in range(4):
-                op("pe", 262, y_op, (m, v, 0), [("qq", 0, mp)], opens=1, name=("y0", m, v), keep=3)
-            for v in range(4):
-                op("pe", 262, y_op, (m, v, 1), [("qq", 1, mp), ("y0", m, v)], name=("y1", m, v))
-                if False:
-                    op("act", 545, y_copy_op, (m, v), [("y1", m, v)], closes=1, name=("yc", m, v))
-                    op("pool", 1270, y_bias_op, (m, v), [("yc", m, v)], name=("ya", m, v))
-                else:
-                    op("dve", 555, y_add_op, (m, v), [("y1", m, v)], closes=1, name=("ya", m, v))
-            w = 1
-            for v in range(0, 4, w):
-                op("sp", 90, y_store_op, (m, v, w), [("ya", m, x) for x in range(v, v + w)], name=("ys", m, v))
+        def step(name, engine, cost, call, after=(), opens=0, frees=0, spare=0):
+            number[name] = len(steps)
+            steps.append((engine, cost, call, [number[x] for x in after], opens, frees, spare))
 
-        for at, key in enumerate(units):
-            j, m0, nm = key
-            n = nm * P
-            half = nm == 2
-            k = 84 * 2 if half else 272
-            room = [("d", units[at - 3])] if at >= 3 else []
-            if at == 0:
-                op("pe", 1, len, ((),), [], opens=6, name=("r", key))
-                for x in ("ch", "cx", "zz", "hT"):
-                    where[x, key] = where["r", key]
-                for jj in (1, 2, 3):
-                    where["hT", (jj, 0, MT)] = where["r", key]
-            elif half:
-                op("pe", 5 * k, mm_op, (key, ("r", "ch")), room, opens=1, name=("r", key))
-                where["ch", key] = where["r", key]
+        PASS, TURN, GPSIMD_COLUMN = 272, 90, 2.4
+
+        def elementwise(columns):
+            return columns + 40
+
+        def plan_sum(name, j, after=()):
+            cost = PASS * len(SUMS[name][1])
+            step((name, j), "tensor", cost, partial(sum_all, name, j), after, opens=1, spare=2 if name == "reset" else 0)
+
+        def plan_run(states_of, news_of, q_of):
+            after = [("new", slab) for slab in news_of]
+            for g, pair in q_of:
+                after += [("q", slab) for slab in WHOLE + HALVES if slab[0] // 4 == g and slab[1] in (0, 2 * pair)]
+            cost = TURN * sum([slab[2] for slab in states_of + news_of] + [4 for pair in q_of])
+            name = ("run", states_of, news_of, q_of)
+            opens = (1 if states_of else 0) + len(news_of) + len(q_of)
+            step(name, "tensor", cost, partial(turn_run, states_of, news_of, q_of), after, opens=opens)
+            for slab in states_of:
+                number["state", slab] = number[name]
+            for slab in news_of:
+                columns = slab[2] * P
+                step(("kept", slab), "scalar", elementwise(columns), partial(keep_new, slab), [name])
+                step(("q", slab), "vector", 2 * elementwise(columns // 2), partial(times_gain, slab), [name, ("kept", slab)], frees=1)
+                if slab[0] % 2 == 1:
+                    before = [x for x in WHOLE + HALVES if x[0] == slab[0] - 1][0]
+                    step(("stored", slab), "scalar", 90, partial(store_new, slab), [("kept", slab), ("kept", before)])
+            for g, pair in q_of:
+                step(("laid", g, pair), "scalar", elementwise(BANK), partial(lay_q, g, pair), [name], frees=1)
+                step(("quantized", g, pair), "vector", elementwise(2 * P), partial(quantize_q, g, pair), [("laid", g, pair)])
+
+        def plan_chain(slab, last_reader):
+            j, columns = slab[0], slab[2] * P
+            frees = 1 if last_reader else 0
+            step(("reset gate", slab), "scalar", elementwise(columns), partial(gate, slab, "reset", RESET), [("reset", j)], frees=frees)
+            step(("rh", slab), "vector", elementwise(columns), partial(reset_hc, slab), [("reset gate", slab), ("hc", j)], frees=frees)
+            step(("pre", slab), "vector", elementwise(columns), partial(add_xc, slab), [("rh", slab), ("xc", j)], frees=frees)
+            step(("cand", slab), "scalar", elementwise(columns), partial(candidate, slab), [("pre", slab)])
+            step(("update gate", slab), "scalar", elementwise(columns), partial(gate, slab, "update", UPDATE), [("update", j)], frees=frees)
+            frees = 1 if slab in LAST_OF_STATE_BANK else 0
+            step(("diff", slab), "vector", elementwise(columns), partial(difference, slab), [("cand", slab), ("state", slab)], frees=frees)
+            if j == LAST:
+                engine, name, cost = nc.vector, "vector", elementwise(columns)
             else:
-                op("pe", 3 * k, mm_op, (key, ("r",)), room, opens=1, name=("r", key))
-                op("pe", 2 * k, mm_op, (key, ("ch",)), [], opens=1, name=("ch", key))
-                op("pe", k, mm_op, (key, ("cx",)), [], opens=1, name=("cx", key))
-            if at in RUNS:
-                states, news = RUNS[at]
-                opens = (1 if states else 0) + len(news)
-                cost = sum([64 * x[2] for x in states] + [85 * x[2] for x in news])
-                op("pe", cost, turns_op, (states, news, ()), [("new", x) for x in news], opens=opens, name=("run", at))
-                for x in states:
-                    where["hT", x] = where["run", at]
-                for x in news:
-                    where["turn_new", x] = where["run", at]
-                    after_turn(x)
-            if half:
-                op("pe", 4 * k, mm_op, (key, ("cx", "z")), [], opens=1, name=("cx", key))
-                where["zz", key] = where["cx", key]
-            elif at > 0:
-                op("pe", 3 * k, mm_op, (key, ("z",)), [], opens=1, name=("zz", key))
-            op("act", n + 40, sig_op, (key, "r", 0), [("r", key)], closes=0 if half else 1, name=("sr", key))
-            op("dve", n + 45, do, (cand_in, key), [("sr", key), ("ch", key)], closes=1, name=("t1", key))
-            op("dve", n + 45, do, (cand_sum, key), [("t1", key), ("cx", key)], closes=0 if half else 1, name=("t2", key))
-            op("act", n + 40, do, (cand_tanh, key), [("t2", key)], name=("cand", key))
-            op("act", n + 40, sig_op, (key, "z", 1), [("zz", key)] + ([("t2", key)] if half else []), closes=1, name=("z", key))
-            op("dve", n + 45, do, (state_diff, key), [("cand", key), ("hT", key)], closes=1 if j % 2 else 0, name=("d", key))
-            for fn, what, needs, on_v in ((state_gate, "e", [("d", key), ("z", key)], m0 == 2), (state_new, "new", [("e", key)], m0 == 2)):
-                eng, name, cost = (VE, "dve", n + 40) if on_v else (G, "pool", 2.4 * n + 40)
-                op(name, cost, do, (fn, key, eng), needs, name=(what, key))
-            if at == 9:
-                q_ops(0, (0, 1), [("q", (jj, 0, MT)) for jj in range(4)])
-        for key in units:
-            if key not in in_run:
-                op("pe", 85 * key[2], turns_op, ((), (key,), ()), [("new", key)], opens=1, name=("turn_new", key))
-                after_turn(key)
-                if key[0] == JT - 1:
-                    q_ops(1, (key[1] // 2,), [("q", (jj, 0, MT) if jj < NF else (jj, key[1], 2)) for jj in range(4, 8)])
-        for m in range(MT):
-            y_ops(m)
+                engine, name, cost = nc.gpsimd, "gpsimd", GPSIMD_COLUMN * columns + 40
+            step(("step", slab), name, cost, partial(times_update, engine, slab), [("diff", slab), ("update gate", slab)])
+            step(("new", slab), name, cost, partial(new_state, engine, slab), [("step", slab)])
 
-        free = {}
-        end = [None] * len(ops)
-        pending = {e: [i for i in range(len(ops)) if ops[i][0] == e] for e in ("pe", "act", "dve", "pool", "sp")}
-        used, release = 0, []
-        order = []
-        while any(pending.values()):
-            best = None
-            for e, queue in pending.items():
-                t0 = free.get(e, 0)
-                pick = None
-                for i in queue:
-                    o = ops[i]
-                    if any(end[x] is None for x in o[4]):
-                        continue
-                    t = max([t0] + [end[x] + (0 if ops[x][0] == e == "pe" else 460 if ops[x][0] == "pe" else 250) for x in o[4]])
-                    spare = 8 - used
-                    if o[5] and spare + len(release) < o[5] + o[7]:
-                        continue
-                    if o[5] > spare:
-                        t = max(t, sorted(release)[o[5] - spare - 1] + 250)
-                    if pick is None or t < pick[0]:
-                        pick = (t, i)
-                    if t == t0:
-                        break
-                if pick and (best is None or pick[0] < best[0]):
-                    best = pick + (e,)
-            t, i, e = best
-            o = ops[i]
-            pending[e].remove(i)
-            order.append(i)
-            if o[5]:
-                short = max(0, o[5] - (8 - used))
-                release = sorted(release)[short:]
-                used += o[5] - short
-            free[e] = t + o[1]
-            end[i] = t + o[1]
-            release += [end[i] + 250] * o[6]
-        for i in order:
-            ops[i][2](*ops[i][3])
+        RUNS = {
+            4: [((WHOLE[4], WHOLE[5]), (WHOLE[0], WHOLE[1]), ())],
+            6: [((WHOLE[6], HALVES[0], HALVES[1]), (WHOLE[2],), ())],
+            7: [((), (WHOLE[3], WHOLE[4]), ()), ((), (), ((0, 0), (0, 1)))],
+        }
+        LAST_RUNS = [
+            ((), (WHOLE[5], WHOLE[6]), ()),
+            ((), (HALVES[0],), ()),
+            ((), (), ((1, 0),)),
+            ((), (HALVES[1],), ()),
+            ((), (), ((1, 1),)),
+        ]
+        LAST_OF_STATE_BANK = (WHOLE[1], WHOLE[3], WHOLE[5], HALVES[1])
+
+        step("head", "tensor", 1, partial(len, ()), opens=len(SUMS) + len(head_banks))
+        for name in SUMS:
+            number[name, 0] = number["head"]
+        for j in range(HEAD_TILES):
+            number["state", WHOLE[j]] = number["head"]
+        for j in range(CHANNEL_TILES):
+            of_tile = [slab for slab in WHOLE + HALVES if slab[0] == j]
+            if j > 0:
+                plan_sum("reset", j, [("diff", WHOLE[j - 4])] if j >= 4 else [])
+                plan_sum("hc", j)
+                plan_sum("xc", j)
+            for run in RUNS.get(j, []):
+                plan_run(*run)
+            if j > 0:
+                plan_sum("update", j)
+            for slab in of_tile:
+                plan_chain(slab, slab == of_tile[-1])
+        for run in LAST_RUNS:
+            plan_run(*run)
+        for m in range(TOKEN_TILES):
+            pair = m // 2
+            for v in range(Y_TILES):
+                step(("y0", m, v), "tensor", PASS, partial(y_pass, m, v, 0), [("quantized", 0, pair)], opens=1, spare=4)
+            for v in range(Y_TILES):
+                step(("y1", m, v), "tensor", PASS, partial(y_pass, m, v, 1), [("quantized", 1, pair), ("y0", m, v)])
+                step(("y", m, v), "vector", elementwise(BANK), partial(y_bias, m, v), [("y1", m, v)], frees=1)
+            for v in range(Y_TILES):
+                step(("stored y", m, v), "sync", 90, partial(y_store, m, v), [("y", m, v)])
+
+        for i in plan_order(steps):
+            steps[i][2]()

from contextlib import ExitStack
from functools import partial

import concourse.mybir as mybir
from concourse.masks import make_identity

F32 = mybir.dt.float32
BF16 = mybir.dt.bfloat16
I32 = mybir.dt.int32
U32 = mybir.dt.uint32
U8 = mybir.dt.uint8
E4M3 = mybir.dt.float8_e4m3fn
E4M3X4 = mybir.dt.float8_e4m3fn_x4
E2M1X4 = mybir.dt.float4_e2m1fn_x4
ACT = mybir.ActivationFunctionType
ALU = mybir.AluOpType

B, D, H, V = 512, 512, 1024, 2048
P = 128
TOKEN_TILES = B // P
CHANNEL_TILES = H // P
BANK = 512
Y_TILES = V // BANK
BANKS = 8
FLOPS = 2 * B * (D * 3 * H + H * 3 * H + H * V)

RESET, UPDATE, CANDIDATE = 0, 1, 2
SUMS = {"reset": (RESET, (0, 1, 2)), "hc": (CANDIDATE, (0, 1)), "xc": (CANDIDATE, (2,)), "update": (UPDATE, (0, 1, 2))}
EARLY_TILES = 2
HEAD_TILES = 4

LAST = CHANNEL_TILES - 1
WHOLE = [(j, 0, TOKEN_TILES) for j in range(LAST)]
HALVES = [(LAST, 0, 2), (LAST, 2, 2)]


def plan_order(steps):
    tensor_lag, lag = 460, 200
    engine_free = {"tensor": 0, "scalar": 0, "vector": 0, "gpsimd": 0, "sync": 0}
    waiting = {engine: [i for i, step in enumerate(steps) if step[0] == engine] for engine in engine_free}
    end = [None] * len(steps)
    taken, returned = 0, []
    order = []
    while any(waiting.values()):
        best = None
        for engine, queue in waiting.items():
            pick = None
            for i in queue:
                after, opens, spare = steps[i][3], steps[i][4], steps[i][6]
                if any(end[x] is None for x in after):
                    continue
                start = engine_free[engine]
                for x in after:
                    on_tensor = steps[x][0] == "tensor"
                    start = max(start, end[x] + (0 if on_tensor and engine == "tensor" else tensor_lag if on_tensor else lag))
                free = BANKS - taken
                if opens and free + len(returned) < opens + spare:
                    continue
                if opens > free:
                    start = max(start, sorted(returned)[opens - free - 1] + lag)
                if pick is None or start < pick[0]:
                    pick = (start, i)
            if pick and (best is None or pick[0] < best[0]):
                best = pick
        start, i = best
        engine, cost, call, after, opens, frees, spare = steps[i]
        waiting[engine].remove(i)
        order.append(i)
        reused = max(0, opens - (BANKS - taken))
        returned = sorted(returned)[reused:]
        taken += opens - reused
        end[i] = engine_free[engine] = start + cost
        returned += [end[i] + lag] * frees
    return order


def tile_gru_candidate_projection_f7_kernel(
    tc, x_bytes, x_scale, h, w_words, w_scales, u_words, u_scales, bias, bias_c, carry, gain, o_words, o_scales, bias_o, out_0, out_1
):
    nc = tc.nc
    with ExitStack() as ctx:
        keep = ctx.enter_context(tc.tile_pool(name="keep", bufs=1))
        work = ctx.enter_context(tc.tile_pool(name="work", bufs=5))
        y_pool = ctx.enter_context(tc.tile_pool(name="y_pool", bufs=3))
        psum = ctx.enter_context(tc.psum_pool(name="psum", bufs=BANKS))
        ctx.enter_context(tc.manual_schedule())

        def new_bank(dtype=F32):
            bank = psum.tile([P, BANK if dtype == F32 else 2 * BANK], dtype, name="bank", tag="bank")
            return bank

        ident = keep.tile([P, P], F32, name="ident")
        ident_bf = keep.tile([P, P], BF16, name="ident_bf")
        warm = keep.tile([P, BANK], BF16, name="warm")
        table = keep.tile([P, 1], F32, name="table")
        vec_rows = keep.tile([P, P], BF16, name="vec_rows")
        vec_cols = keep.tile([P, 6 * CHANNEL_TILES], F32, name="vec_cols")
        gain_cols = keep.tile([P, CHANNEL_TILES], BF16, name="gain_cols")
        gain_all = keep.tile([P, H], BF16, name="gain_all")
        bias_o_all = keep.tile([P, V], BF16, name="bias_o_all")
        x_codes = keep.tile([P, TOKEN_TILES, D], U8, name="x_codes", align_bytes=64)
        x_wide = keep.tile([P, TOKEN_TILES, D], BF16, name="x_wide", align_bytes=64)
        x_scale_4 = keep.tile([P, 4], F32, name="x_scale_4")
        h_rows = keep.tile([P, TOKEN_TILES, H], BF16, name="h_rows", align_bytes=64)
        words_early = keep.tile([P, 3, 3, EARLY_TILES * P * 2], U8, name="words_early", align_bytes=256)
        words_late = keep.tile([P, 3, 3, (CHANNEL_TILES - EARLY_TILES) * P * 2], U8, name="words_late", align_bytes=256)
        u_bytes = keep.tile([P, 2, 3 * H], U8, name="u_bytes", align_bytes=256)
        w_bytes = keep.tile([P, 3 * H], U8, name="w_bytes", align_bytes=256)
        o_codes = keep.tile([P, 2, V * 4], U8, name="o_codes", align_bytes=256)
        o_bytes = keep.tile([P, 2, V], U8, name="o_bytes", align_bytes=256)
        h_in = keep.tile([P, 2, B, 4], BF16, name="h_in", align_bytes=64)
        x_in = keep.tile([P, B, 4], BF16, name="x_in", align_bytes=64)
        q_in = keep.tile([P, 2, B, 4], BF16, name="q_in", align_bytes=64)
        hx_codes = keep.tile([P, 3, B], U32, name="hx_codes", align_bytes=256)
        hx_bytes = keep.tile([P, 3, B], U8, name="hx_bytes", align_bytes=256)
        q_codes = keep.tile([P, 2, B], U32, name="q_codes", align_bytes=256)
        q_bytes = keep.tile([P, 2, B], U8, name="q_bytes", align_bytes=256)
        new_rows = keep.tile([P, TOKEN_TILES, H], F32, name="new_rows")
        q_rows = keep.tile([P, TOKEN_TILES, 2, 2, P, 2], BF16, name="q_rows", align_bytes=64)

        nc.vector.memset(table[:], 0.0)
        nc.vector.memset(warm[:], 0.0)
        nc.vector.memset(vec_rows[:], 0.0)
        nc.vector.memset(u_bytes[:].rearrange("p g n -> p (g n)").bitcast(I32), 0)
        nc.vector.memset(w_bytes[:].bitcast(I32), 0)
        nc.vector.memset(o_bytes[:].rearrange("p g n -> p (g n)").bitcast(I32), 0)
        make_identity(nc, ident[:])
        nc.gpsimd.tensor_copy(out=ident_bf[:], in_=ident[:])
        first_row = 0
        for vector in (gain, bias, bias_c, carry):
            rows = vector.shape[0] // P
            nc.gpsimd.dma_start(out=vec_rows[first_row : first_row + rows, :], in_=vector.rearrange("(r c) -> r c", c=P))
            first_row += rows

        h_view = h.rearrange("(m p) d -> p m d", p=P)

        def load_words(tile, first, last, groups):
            for g in groups:
                source = u_words[g] if g < 2 else w_words[0]
                part_view = source.rearrange("p (part n) -> p part n", part=3)
                nc.sync.dma_start(out=tile[:, g, :, :], in_=part_view[:, :, first * 2 * P : last * 2 * P])

        def load_scale_rows(tile_rows, scales):
            view = scales.rearrange("g (b r) n -> r b g n", r=4)
            for r in range(4):
                nc.sync.dma_start(out=tile_rows[r:P:32, :, :].bitcast(I32), in_=view[r].bitcast(I32))

        nc.sync.dma_start(out=h_rows[:, 0, :], in_=h_view[:, 0, :])
        nc.sync.dma_start(out=x_codes[:], in_=x_bytes.rearrange("(m p) d -> p m d", p=P))
        nc.sync.dma_start(out=h_rows[:, 1, :], in_=h_view[:, 1, :])
        nc.scalar.dma_start(out=x_scale_4[:], in_=x_scale.rearrange("o (p t) -> p (o t)", t=4))
        nc.scalar.activation(out=table[:], in_=table[:], func=ACT.Sigmoid)
        load_scale_rows(u_bytes, u_scales)
        load_words(words_early, 0, EARLY_TILES, (0, 1, 2))
        nc.sync.dma_start(out=h_rows[:, 2:4, :], in_=h_view[:, 2:4, :])
        load_scale_rows(w_bytes[:].rearrange("p (o n) -> p o n", o=1), w_scales)
        load_words(words_late, EARLY_TILES, CHANNEL_TILES, (0, 1, 2))
        load_scale_rows(o_bytes, o_scales)
        for g in range(2):
            o_view = o_words[g].rearrange("p n t -> p (n t)")
            for half in range(2):
                cols = slice(half * 2 * V, (half + 1) * 2 * V)
                nc.sync.dma_start(out=o_codes[:, g, cols].bitcast(I32), in_=o_view[:, cols].bitcast(I32))
        nc.sync.dma_start(out=bias_o_all[:], in_=bias_o.partition_broadcast(P))

        def turn_h(m):
            bank = new_bank()
            words = h_rows[:, m, :].bitcast(F32)
            for g in range(2):
                for u in range(2):
                    i = 2 * g + u
                    nc.tensor.transpose(bank[:, i * P : (i + 1) * P], words[:, 256 * g + u : 256 * (g + 1) : 2], ident[:])
            return bank

        def lay_h(m, bank, copy):
            words = h_in[:].rearrange("p g r t -> p g (r t)").bitcast(F32)
            to = words[:, :, m * 2 * P : (m + 1) * 2 * P].rearrange("p g (r u) -> p g r u", u=2)
            copy(out=to, in_=bank[:].rearrange("p (g u r) -> p g r u", g=2, u=2))

        def quantize_h(m):
            tokens = slice(m * P, (m + 1) * P)
            for g in range(2):
                nc.vector.quantize_mx(
                    out=hx_codes[:, g, tokens].bitcast(E4M3X4),
                    scales=hx_bytes[:, g, tokens],
                    in_=h_in[:, g, tokens, :].rearrange("p r t -> p (r t)"),
                )

        def turn_x(pair):
            bank = new_bank()
            for m in range(2):
                words = x_wide[:, 2 * pair + m, :].bitcast(F32)
                for u in range(2):
                    i = 2 * m + u
                    nc.tensor.transpose(bank[:, i * P : (i + 1) * P], words[:, u : 2 * P : 2], ident[:])
            return bank

        def scale_x(pair, bank):
            scales = x_scale_4[:].rearrange("p (u e) -> p u e", e=2).unsqueeze(1).to_broadcast([P, P, 2, 2])
            for m in range(2):
                first = (2 * pair + m) * P
                nc.vector.tensor_tensor(
                    out=x_in[:, first : first + P, :].rearrange("p r (u e) -> p r u e", e=2),
                    in0=bank[:, 2 * P * m : 2 * P * (m + 1)].bitcast(BF16).rearrange("p (u r e) -> p r u e", u=2, e=2),
                    in1=scales,
                    op=ALU.mult,
                )

        def quantize_x(pair):
            tokens = slice(pair * 2 * P, (pair + 1) * 2 * P)
            nc.vector.quantize_mx(
                out=hx_codes[:, 2, tokens].bitcast(E4M3X4),
                scales=hx_bytes[:, 2, tokens],
                in_=x_in[:, tokens, :].rearrange("p r t -> p (r t)"),
            )

        def column(vector, j):
            i = (vector + 1) * CHANNEL_TILES + j
            return vec_cols[:, i : i + 1]

        BIAS_C, CARRY = 3, 4

        def sum_passes(out, name, j, tokens):
            part, groups = SUMS[name]
            c = part * H + j * P
            for g in groups:
                tile, first = (words_early, j) if j < EARLY_TILES else (words_late, j - EARLY_TILES)
                nc.tensor.matmul_mx(
                    out=out,
                    lhsT=tile[:, g, part, first * 2 * P : (first + 1) * 2 * P].bitcast(E2M1X4),
                    lhsT_scale=u_bytes[:, g, c : c + P] if g < 2 else w_bytes[:, c : c + P],
                    rhs=hx_codes[:, g, tokens].bitcast(E4M3X4),
                    rhs_scale=hx_bytes[:, g, tokens],
                    start=(g == groups[0]),
                    stop=(g == groups[-1]),
                )

        sums = {}
        states = {}
        slabs = {}

        def sum_all(name, j):
            sums[name, j] = new_bank()
            sum_passes(sums[name, j][:], name, j, slice(0, B))

        def of(slab, name):
            tiles = slabs.setdefault(slab, {})
            if name not in tiles:
                tiles[name] = work.tile([P, B], F32, name=name, tag=name)
            return tiles[name][:, 0 : slab[2] * P]

        def sum_of(slab, name):
            return sums[name, slab[0]][:, slab[1] * P : (slab[1] + slab[2]) * P]

        def gate(slab, name, part):
            nc.scalar.activation(out=of(slab, name), in_=sum_of(slab, name), func=ACT.Sigmoid, bias=column(part, slab[0]))

        def reset_hc(slab):
            nc.vector.scalar_tensor_tensor(
                out=of(slab, "rh"), in0=sum_of(slab, "hc"), scalar=column(BIAS_C, slab[0]), in1=of(slab, "reset"), op0=ALU.add, op1=ALU.mult
            )

        def add_xc(slab):
            nc.vector.tensor_tensor(out=of(slab, "pre"), in0=sum_of(slab, "xc"), in1=of(slab, "rh"), op=ALU.add)

        def candidate(slab):
            nc.scalar.activation(out=of(slab, "cand"), in_=of(slab, "pre"), func=ACT.Tanh, bias=column(CANDIDATE, slab[0]))

        def difference(slab):
            nc.vector.scalar_tensor_tensor(
                out=of(slab, "diff"), in0=states[slab], scalar=column(CARRY, slab[0]), in1=of(slab, "cand"), op0=ALU.mult, op1=ALU.subtract
            )

        def times_update(engine, slab):
            engine.tensor_tensor(out=of(slab, "step"), in0=of(slab, "update"), in1=of(slab, "diff"), op=ALU.mult)

        def new_state(engine, slab):
            engine.tensor_tensor(out=of(slab, "new"), in0=of(slab, "cand"), in1=of(slab, "step"), op=ALU.add)

        def turn_state(out, j, m):
            nc.tensor.transpose(out, h_rows[:, m, j * P : (j + 1) * P], ident_bf[:])

        turned = {}
        q_banks = {}
        new_view = out_1.rearrange("(m p) c -> p m c", p=P)
        y_view = out_0.rearrange("(m p) v -> p m v", p=P)

        def turn_run(states_of, news_of, q_of):
            if states_of:
                bank = new_bank(BF16)
                at = 0
                for slab in states_of:
                    states[slab] = bank[:, at : at + slab[2] * P]
                    for m in range(slab[1], slab[1] + slab[2]):
                        turn_state(bank[:, at : at + P], slab[0], m)
                        at += P
            for slab in news_of:
                bank = new_bank()
                for m in range(slab[2]):
                    nc.tensor.transpose(bank[:, m * P : (m + 1) * P], of(slab, "new")[:, m * P : (m + 1) * P], ident[:])
                turned[slab] = bank[:, 0 : slab[2] * P].rearrange("p (m c) -> p m c", c=P)
            for g, pair in q_of:
                bank = new_bank()
                for m in range(2):
                    for u in range(2):
                        i = 2 * m + u
                        words = q_rows[:, 2 * pair + m, g, u, :, :].rearrange("p k e -> p (k e)").bitcast(F32)
                        nc.tensor.transpose(bank[:, i * P : (i + 1) * P], words, ident[:])
                q_banks[g, pair] = bank

        def keep_new(slab):
            j, m, n = slab
            nc.scalar.copy(out=new_rows[:, m : m + n, j * P : (j + 1) * P], in_=turned[slab])

        def times_gain(slab):
            j, m, n = slab
            g, first = j // 4, j % 4 * (P // 4)
            by_u = turned[slab].rearrange("p m (k u e) -> p m u k e", u=2, e=2)
            gain_by_u = gain_all[:, j * P : (j + 1) * P].rearrange("p (k u e) -> p u k e", u=2, e=2)
            for u in range(2):
                nc.vector.tensor_tensor(
                    out=q_rows[:, m : m + n, g, u, first : first + P // 4, :],
                    in0=by_u[:, :, u, :, :],
                    in1=gain_by_u[:, u, :, :].unsqueeze(1).to_broadcast([P, n, P // 4, 2]),
                    op=ALU.mult,
                )

        def lay_q(g, pair):
            words = q_in[:].rearrange("p g r t -> p g (r t)").bitcast(F32)
            to = words[:, g, pair * 4 * P : (pair + 1) * 4 * P].rearrange("p (m r u) -> p m r u", m=2, u=2)
            nc.scalar.copy(out=to, in_=q_banks[g, pair][:].rearrange("p (m u r) -> p m r u", m=2, u=2))

        def quantize_q(g, pair):
            tokens = slice(pair * 2 * P, (pair + 1) * 2 * P)
            nc.vector.quantize_mx(
                out=q_codes[:, g, tokens].bitcast(E4M3X4),
                scales=q_bytes[:, g, tokens],
                in_=q_in[:, g, tokens, :].rearrange("p r t -> p (r t)"),
            )

        def store_new(slab):
            j, m, n = slab
            cols = slice((j - 1) * P, (j + 1) * P)
            nc.scalar.dma_start(out=new_view[:, m : m + n, cols], in_=new_rows[:, m : m + n, cols])

        y_banks = {}
        y_rows = {}

        def y_pass(m, v, g):
            if g == 0:
                y_banks[m, v] = new_bank()
            tokens = slice(m * P, (m + 1) * P)
            nc.tensor.matmul_mx(
                out=y_banks[m, v][:],
                lhsT=q_codes[:, g, tokens].bitcast(E4M3X4),
                lhsT_scale=q_bytes[:, g, tokens],
                rhs=o_codes[:, g, v * 4 * BANK : (v + 1) * 4 * BANK].bitcast(E4M3X4),
                rhs_scale=o_bytes[:, g, v * BANK : (v + 1) * BANK],
                start=(g == 0),
                stop=(g == 1),
            )

        def y_bias(m, v):
            if m not in y_rows:
                y_row = y_pool.tile([P, V], F32, name="y_row")
                y_rows[m] = y_row
            cols = slice(v * BANK, (v + 1) * BANK)
            nc.vector.tensor_tensor(out=y_rows[m][:, cols], in0=y_banks[m, v][:], in1=bias_o_all[:, cols], op=ALU.add)

        def y_store(m, v):
            cols = slice(v * BANK, (v + 1) * BANK)
            nc.sync.dma_start(out=y_view[:, m, cols], in_=y_rows[m][:, cols])

        head_banks = [new_bank(BF16), new_bank(BF16)]

        def turn_head_states(ms):
            for j in range(HEAD_TILES):
                state = head_banks[j // 2][:, j % 2 * B : (j % 2 + 1) * B]
                states[j, 0, TOKEN_TILES] = state
                for m in ms:
                    turn_state(state[:, m * P : (m + 1) * P], j, m)

        def first_sums(ms):
            for m in ms:
                for name in ("hc", "reset", "xc", "update"):
                    if (name, 0) not in sums:
                        sums[name, 0] = new_bank()
                    tokens = slice(m * P, (m + 1) * P)
                    sum_passes(sums[name, 0][:, tokens], name, 0, tokens)

        def warm_up(passes):
            bank = new_bank()
            for i in range(passes):
                nc.tensor.matmul(bank[:], lhsT=warm[:, 0:P], rhs=warm[:], start=True, stop=True)

        scalar_copy, vector_copy = nc.scalar.copy, nc.vector.tensor_copy
        warm_up(4)
        h_bank = turn_h(0)
        lay_h(0, h_bank, scalar_copy)
        for m in range(TOKEN_TILES):
            nc.vector.tensor_copy(out=x_wide[:, m, :], in_=x_codes[:, m, :].bitcast(E4M3))
        warm_up(1)
        x_banks = [turn_x(0), turn_x(1)]
        h_bank = turn_h(1)
        quantize_h(0)
        scale_x(0, x_banks[0])
        lay_h(1, h_bank, scalar_copy)
        quantize_x(0)
        quantize_h(1)
        scale_x(1, x_banks[1])
        turn_head_states((0, 1))
        first_sums((0, 1))
        vec_bank = new_bank(BF16)
        nc.tensor.transpose(vec_bank[:, 0:P], vec_rows[:], ident_bf[:])
        nc.scalar.copy(out=gain_cols[:], in_=vec_bank[:, 0:CHANNEL_TILES])
        nc.scalar.copy(out=vec_cols[:], in_=vec_bank[:, 0 : 6 * CHANNEL_TILES])
        h_banks = [turn_h(2), turn_h(3)]
        lay_h(2, h_banks[0], scalar_copy)
        quantize_x(1)
        lay_h(3, h_banks[1], vector_copy)
        quantize_h(2)
        quantize_h(3)
        turn_head_states((2, 3))
        gain_banks = [new_bank(), new_bank()]
        for j in range(CHANNEL_TILES):
            nc.tensor.matmul(
                gain_banks[j // 4][:, j % 4 * P : (j % 4 + 1) * P],
                lhsT=gain_cols[:, j : j + 1].to_broadcast([P, P]),
                rhs=ident_bf[:],
                start=True,
                stop=True,
            )
        first_sums((2, 3))
        for i in range(2):
            nc.scalar.copy(out=gain_all[:, i * BANK : (i + 1) * BANK], in_=gain_banks[i][:])

        steps = []
        number = {}

        def step(name, engine, cost, call, after=(), opens=0, frees=0, spare=0):
            number[name] = len(steps)
            steps.append((engine, cost, call, [number[x] for x in after], opens, frees, spare))

        PASS, TURN, GPSIMD_COLUMN = 272, 90, 2.4

        def elementwise(columns):
            return columns + 40

        def plan_sum(name, j, after=()):
            cost = PASS * len(SUMS[name][1])
            step((name, j), "tensor", cost, partial(sum_all, name, j), after, opens=1, spare=2 if name == "reset" else 0)

        def plan_run(states_of, news_of, q_of):
            after = [("new", slab) for slab in news_of]
            for g, pair in q_of:
                after += [("q", slab) for slab in WHOLE + HALVES if slab[0] // 4 == g and slab[1] in (0, 2 * pair)]
            cost = TURN * sum([slab[2] for slab in states_of + news_of] + [4 for pair in q_of])
            name = ("run", states_of, news_of, q_of)
            opens = (1 if states_of else 0) + len(news_of) + len(q_of)
            step(name, "tensor", cost, partial(turn_run, states_of, news_of, q_of), after, opens=opens)
            for slab in states_of:
                number["state", slab] = number[name]
            for slab in news_of:
                columns = slab[2] * P
                step(("kept", slab), "scalar", elementwise(columns), partial(keep_new, slab), [name])
                step(("q", slab), "vector", 2 * elementwise(columns // 2), partial(times_gain, slab), [name, ("kept", slab)], frees=1)
                if slab[0] % 2 == 1:
                    before = [x for x in WHOLE + HALVES if x[0] == slab[0] - 1][0]
                    step(("stored", slab), "scalar", 90, partial(store_new, slab), [("kept", slab), ("kept", before)])
            for g, pair in q_of:
                step(("laid", g, pair), "scalar", elementwise(BANK), partial(lay_q, g, pair), [name], frees=1)
                step(("quantized", g, pair), "vector", elementwise(2 * P), partial(quantize_q, g, pair), [("laid", g, pair)])

        def plan_chain(slab, last_reader):
            j, columns = slab[0], slab[2] * P
            frees = 1 if last_reader else 0
            step(("reset gate", slab), "scalar", elementwise(columns), partial(gate, slab, "reset", RESET), [("reset", j)], frees=frees)
            step(("rh", slab), "vector", elementwise(columns), partial(reset_hc, slab), [("reset gate", slab), ("hc", j)], frees=frees)
            step(("pre", slab), "vector", elementwise(columns), partial(add_xc, slab), [("rh", slab), ("xc", j)], frees=frees)
            step(("cand", slab), "scalar", elementwise(columns), partial(candidate, slab), [("pre", slab)])
            step(("update gate", slab), "scalar", elementwise(columns), partial(gate, slab, "update", UPDATE), [("update", j)], frees=frees)
            frees = 1 if slab in LAST_OF_STATE_BANK else 0
            step(("diff", slab), "vector", elementwise(columns), partial(difference, slab), [("cand", slab), ("state", slab)], frees=frees)
            if j == LAST:
                engine, name, cost = nc.vector, "vector", elementwise(columns)
            else:
                engine, name, cost = nc.gpsimd, "gpsimd", GPSIMD_COLUMN * columns + 40
            step(("step", slab), name, cost, partial(times_update, engine, slab), [("diff", slab), ("update gate", slab)])
            step(("new", slab), name, cost, partial(new_state, engine, slab), [("step", slab)])

        RUNS = {
            4: [((WHOLE[4], WHOLE[5]), (WHOLE[0], WHOLE[1]), ())],
            6: [((WHOLE[6], HALVES[0], HALVES[1]), (WHOLE[2],), ())],
            7: [((), (WHOLE[3], WHOLE[4]), ()), ((), (), ((0, 0), (0, 1)))],
        }
        LAST_RUNS = [
            ((), (WHOLE[5], WHOLE[6]), ()),
            ((), (HALVES[0],), ()),
            ((), (), ((1, 0),)),
            ((), (HALVES[1],), ()),
            ((), (), ((1, 1),)),
        ]
        LAST_OF_STATE_BANK = (WHOLE[1], WHOLE[3], WHOLE[5], HALVES[1])

        step("head", "tensor", 1, partial(len, ()), opens=len(SUMS) + len(head_banks))
        for name in SUMS:
            number[name, 0] = number["head"]
        for j in range(HEAD_TILES):
            number["state", WHOLE[j]] = number["head"]
        for j in range(CHANNEL_TILES):
            of_tile = [slab for slab in WHOLE + HALVES if slab[0] == j]
            if j > 0:
                plan_sum("reset", j, [("diff", WHOLE[j - 4])] if j >= 4 else [])
                plan_sum("hc", j)
                plan_sum("xc", j)
            for run in RUNS.get(j, []):
                plan_run(*run)
            if j > 0:
                plan_sum("update", j)
            for slab in of_tile:
                plan_chain(slab, slab == of_tile[-1])
        for run in LAST_RUNS:
            plan_run(*run)
        for m in range(TOKEN_TILES):
            pair = m // 2
            for v in range(Y_TILES):
                step(("y0", m, v), "tensor", PASS, partial(y_pass, m, v, 0), [("quantized", 0, pair)], opens=1, spare=4)
            for v in range(Y_TILES):
                step(("y1", m, v), "tensor", PASS, partial(y_pass, m, v, 1), [("quantized", 1, pair), ("y0", m, v)])
                step(("y", m, v), "vector", elementwise(BANK), partial(y_bias, m, v), [("y1", m, v)], frees=1)
            for v in range(Y_TILES):
                step(("stored y", m, v), "sync", 90, partial(y_store, m, v), [("y", m, v)])

        for i in plan_order(steps):
            steps[i][2]()
